import numpy as np, ml_dtypes
CORES = [6,14,30,38,62,70,86,94,102]
N = 9
S, T = 16384, 2048
def entries(a): return a.T.reshape(-1)
def pack(v, P): return np.ascontiguousarray(np.asarray(v, np.int32).reshape(-1, P).T)
def lists(rng, how):
    M = rng.integers(0, S, (N, S)); b = rng.integers(0, S, T)
    if how == "alike": M = np.stack([rng.permutation(S) for f in range(N)]); b[:] = rng.integers(S)
    if how == "edge":
        M = np.where(rng.random((N, S)) < 0.5, 0, S - 1); w = rng.permutation(N) % 2 * (S - 1); M[:, 0] = w; M[:, S - 1] = S - 1 - w
        b = np.where(rng.random(T) < 0.5, 0, S - 1); b[rng.permutation(T)[:2]] = [0, S - 1]
    if how == "fold":
        V = np.stack([rng.permutation(S)[:4] for f in range(N + 1)]); M = V[np.arange(N)[:, None], rng.integers(0, 4, (N, S))]
        M[np.arange(N)[:, None], V[1:]] = V[:N]; b[rng.permutation(T)[:4]] = V[N]
    if how == "mixed":
        k = np.concatenate([[3, 3], rng.permutation(np.arange(N - 2) % 3)])
        for f in range(N): M[f] = [np.arange(S), rng.permutation(S), M[f], rng.integers(0, S, 4)[rng.integers(0, 4, S)]][k[f]]
    if how == "turn": M = np.stack([rng.permutation(S) for f in range(N)]); b = rng.permutation(S)[:T]
    return {"bp": np.stack([pack(m, 16) for m in M]), "st": np.broadcast_to(pack(b, 16), (N, 16, T // 16)).copy()}
def setup_inputs(rng):
    return dict({"tab": rng.standard_normal((N, 128, S), dtype=np.float32).astype(ml_dtypes.bfloat16)}, **lists(rng, "uniform"))
def setup_inputs_alike(rng):
    d = setup_inputs(rng); d.update(lists(rng, "alike"))
    for k in ("tab",): d[k] = (d[k].astype(np.float32) * 1048576.0).astype(d[k].dtype)
    return d
def setup_inputs_edge(rng):
    d = setup_inputs(rng); d.update(lists(rng, "edge"))
    for k in ("tab",): d[k] = (d[k].astype(np.float32) * (1 / 1024.0)).astype(d[k].dtype)
    return d
def setup_inputs_fold(rng):
    d = setup_inputs(rng); d.update(lists(rng, "fold"))
    return d
def setup_inputs_mixed(rng):
    d = setup_inputs(rng); d.update(lists(rng, "mixed"))
    return d
def setup_inputs_turn(rng):
    d = setup_inputs(rng); d.update(lists(rng, "turn"))
    return d
def check_inputs(x):
    bad = []
    if x["bp"].min() < 0 or x["bp"].max() >= S: bad.append("bp out of range")
    if x["st"].min() < 0 or x["st"].max() >= S: bad.append("st out of range")
    if not all(np.array_equal(a, x["st"][0]) for a in x["st"]): bad.append("st isn't alike on all ranks")
    return bad
def reference(tab, bp, st):
    b = entries(st[0]); y = np.zeros((N, 128, T), tab.dtype)
    for f in range(N - 1, -1, -1):
        y[f] = tab[f][:, b]
        b = entries(bp[f])[b]
    return {"y": y}

@@ -1,0 +1,320 @@
+from concourse.bass import DstId, RemoteDMATransfer
+from concourse.mybir import AluOpType, ActivationFunctionType
+
+N = 9
+NCORES = 112
+Q = 4
+NB = 4
+STEPS = N - 1
+SW = 264
+FIN = 256
+FIRST = 2048
+
+SCRATCH = {
+    "tabw": ("sbuf", [128, 16384], "bfloat16"),
+    "yb": ("sbuf", [128, 2048], "bfloat16"),
+    "vb": ("sbuf", [128, 132], "int32"),
+    "u": ("sbuf", [128, 132], "int32"),
+    "t1": ("sbuf", [128, 132], "int32"),
+    "t2": ("sbuf", [128, 132], "int32"),
+    "lab": ("sbuf", [128, 132], "int32"),
+    "wout": ("sbuf", [128, 256], "bfloat16"),
+    "sti": ("sbuf", [128, 16], "int32"),
+    "lst0": ("sbuf", [128, 32], "float32"),
+    "st8": ("sbuf", [128, 128], "int32"),
+    "land": ("sbuf", [128, 32], "float32"),
+    "hh": ("sbuf", [128, 16], "int32"),
+    "hf": ("sbuf", [128, 16], "float32"),
+    "wsum": ("sbuf", [128, 16], "float32"),
+    "sval": ("sbuf", [128, 16], "float32"),
+    "xsp": ("sbuf", [128, 128], "float32"),
+    "e1": ("sbuf", [128, 128], "float32"),
+    "e2": ("sbuf", [128, 128], "float32"),
+    "e3": ("sbuf", [128, 128], "float32"),
+    "ji": ("sbuf", [128, 128], "int32"),
+    "ja": ("sbuf", [128, 128], "int32"),
+    "jm": ("sbuf", [128, 128], "float32"),
+    "pi": ("sbuf", [128, 8], "int32"),
+    "pa": ("sbuf", [128, 8], "int32"),
+    "coffs": ("sbuf", [128, 8], "uint16"),
+    "offs": ("sbuf", [128, 128], "uint16"),
+    "ones": ("sbuf", [128, 128], "bfloat16"),
+    "ident": ("sbuf", [128, 128], "bfloat16"),
+    "col": ("sbuf", [128, 128], "bfloat16"),
+    "lam": ("sbuf", [128, 128], "bfloat16"),
+    "win": ("sbuf", [128, 256 * N], "bfloat16"),
+    "S": ("sbuf", [128, SW * (STEPS + 1)], "float32"),
+}
+for _b in range(NB):
+    SCRATCH["O%d" % _b] = ("sbuf", [128, 128], "bfloat16")
+    SCRATCH["A%d" % _b] = ("sbuf", [128, 128], "bfloat16")
+    SCRATCH["M%d" % _b] = ("sbuf", [128, 128], "bfloat16")
+    SCRATCH["P%d" % _b] = ("psum", [128, 1024], "bfloat16")
+    SCRATCH["R%d" % _b] = ("psum", [128, 512], "float32")
+
+SEMAPHORES = (["ldb", "ldt", "lds", "v", "enc", "snt", "lin", "g1", "g2", "g3", "g4", "mm", "xr", "ofr", "sto",
+               "st0", "k1", "k2", "k3", "k4", "yd0", "yd1", "yd2", "yd3"]
+              + ["map%d" % f for f in range(1, N)]
+              + ["%s%d" % (k, b) for k in ("O", "P", "A", "M", "R", "S", "F") for b in range(NB)])
+
+
+def walkers(T, topo):
+    ranks = list(T.cores)
+    used = [topo.chip(c) for c in ranks]
+    planes = []
+    seen = []
+    for c in range(NCORES):
+        ch = topo.chip(c)
+        if ch in used or ch in seen or topo.die(c) != topo.die(ranks[0]):
+            continue
+        if not all(topo.may_write(c, r) for r in ranks):
+            continue
+        seen.append(ch)
+        for pl in planes:
+            if topo.same_plane(topo.chip(pl[0]), ch):
+                pl.append(c)
+                break
+        else:
+            planes.append([c])
+    out = []
+    i = 0
+    while len(out) < Q:
+        for pl in planes:
+            if i < len(pl) and len(out) < Q:
+                out.append(pl[i])
+        i += 1
+    return out
+
+
+def stile(T, t, a, b, step=1):
+    return T.S[:, SW * t + a:SW * t + b:step]
+
+
+def window(T, f):
+    return T.win[:, 256 * f:256 * f + 256]
+
+
+def bits(m):
+    return [1 << i for i in range(16) if m >> i & 1]
+
+
+def shares(src, dsts, topo):
+    m = topo.mask(src, dsts[0])
+    for d in dsts:
+        m &= topo.mask(src, d)
+    e = bits(m)
+    n = len(e) // len(dsts)
+    return [sum(e[i * n:(i + 1) * n]) for i in range(len(dsts))], n
+
+
+def fused(g, core, topo, dsts, srcs, outs, rsem, lsem):
+    masks, n = shares(core, dsts, topo)
+    tr = []
+    for d, m, s, o in zip(dsts, masks, srcs, outs):
+        rid, pid, _ = topo.addr(d)
+        tr.append(RemoteDMATransfer(dst_ids=[DstId(rid=rid, pnc=pid)], dma_engine_mask=m, remote_sem=rsem,
+                                    srcs=[s], dsts=[o], alu_op=0))
+    g.remote_dma_fused(tr, local_sem=lsem)
+    return n * len(dsts)
+
+
+def rank_program(g, core, T, topo):
+    walk = walkers(T, topo)
+    rank = T.rank_of(core)
+    if rank is not None:
+        run_rank(g, core, rank, T, topo, walk)
+    elif core in walk:
+        run_walker(g, core, walk.index(core), T, topo, walk)
+
+
+def run_walker(g, core, q, T, topo, walk):
+    sem = T.sem
+    v, a, pe = g.vector, g.scalar, g.tensor
+    op = AluOpType
+    SS = [FIN + 7 - 2 * b for b in range(NB)]
+    SO = [FIN + 6 - 2 * b for b in range(NB)]
+    n_in = shares(T.cores[0], walk, topo)[1]
+
+    v.memset(T.ones[:], 1.0).then_inc(sem["k1"], 1)
+    fl = dict(allow_small_or_imprecise_dtypes=True)
+    g.iota(T.lam[:], [[1, 16], [16, 8]], 0, 0, **fl).then_inc(sem["k3"], 1)
+    g.iota(T.col[:], [[1, 128]], 0, 0, **fl).then_inc(sem["k4"], 1)
+    g.wait_ge(sem["k1"], 1)
+    g.affine_select(T.ident[:], T.ones[:], [[-1, 128]], op.is_equal, 0.0, 0, 1).then_inc(sem["k2"], 1)
+
+    def onehot(t, b):
+        v.tensor_scalar(T["O%d" % b][:], T.lam[:], stile(T, t - 1, SS[b], SS[b] + 1), None,
+                        op.is_equal).then_inc(sem["O%d" % b], 1)
+
+    v.wait_ge(sem["k3"], 1)
+    v.wait_ge(sem["st0"], n_in)
+    for b in range(NB):
+        onehot(1, b)
+    for t in range(1, STEPS + 1):
+        for b in range(NB):
+            A, R = T["A%d" % b], T["R%d" % b]
+            v.wait_ge(sem["A%d" % b], t)
+            v.wait_ge(sem["R%d" % b], t)
+            if b > 0:
+                v.wait_ge(sem["S%d" % (b - 1)], t)
+            v.tensor_tensor_scan(stile(T, t, SS[b] - 254, SS[b] + 1, 2), A[:], R[:, 0:128], 0.0, op.mult,
+                                 op.add).then_inc(sem["S%d" % b], 1)
+            if b > 0:
+                v.wait_ge(sem["F%d" % (b - 1)], t)
+            v.tensor_tensor_scan(stile(T, t, SO[b] - 254, SO[b] + 1, 2), A[:], R[:, 128:256], 0.0, op.mult,
+                                 op.add).then_inc(sem["F%d" % b], 1)
+            if t < STEPS:
+                v.wait_ge(sem["S%d" % b], t)
+                onehot(t + 1, b)
+
+    a.wait_ge(sem["k4"], 1)
+    a.wait_ge(sem["st0"], n_in)
+    for t in range(1, STEPS + 1):
+        for b in range(NB):
+            if t > 1:
+                a.wait_ge(sem["S%d" % b], t - 1)
+                a.wait_ge(sem["F%d" % b], t - 1)
+            a.activation(T["A%d" % b][:], T.col[:], ActivationFunctionType.Sign,
+                         bias=stile(T, t - 1, SO[b], SO[b] + 1), scale=16.0).then_inc(sem["A%d" % b], 1)
+            a.wait_ge(sem["P%d" % b], t)
+            a.activation(T["M%d" % b][:], T["P%d" % b][:, 0:128],
+                         ActivationFunctionType.Copy).then_inc(sem["M%d" % b], 1)
+
+    def turn(k):
+        t, b = k // NB + 1, k % NB
+        pe.wait_ge(sem["O%d" % b], t)
+        pe.transpose(T["P%d" % b][:, 0:128], T["O%d" % b][:], T.ident[:]).then_inc(sem["P%d" % b], 1)
+
+    pe.wait_ge(sem["k2"], 1)
+    turn(0)
+    for k in range(STEPS * NB):
+        t, b = k // NB + 1, k % NB
+        if k + 1 < STEPS * NB:
+            turn(k + 1)
+        f = N - t
+        if b == 0:
+            pe.wait_ge(sem["map%d" % f], n_in)
+        pe.wait_ge(sem["M%d" % b], t)
+        pe.matmul(T["R%d" % b][:, 0:256], T["M%d" % b][:], window(T, f), True, True).then_inc(sem["R%d" % b], 1)
+
+    sent = 0
+    for t in range(1, STEPS + 1):
+        for b in range(NB):
+            g.wait_ge(sem["S%d" % b], t)
+            g.wait_ge(sem["F%d" % b], t)
+        dst = T.cores[N - 1 - t]
+        m = topo.mask(core, dst)
+        rid, pid, _ = topo.addr(dst)
+        g.remote_dma(T.land[:, 8 * q:8 * q + 8], stile(T, t, FIN, FIN + 8), sem["lin"], sem["snt"], pid, rid, m)
+        sent += len(bits(m))
+    g.wait_ge(sem["snt"], sent)
+
+
+def run_rank(g, core, rank, T, topo, walk):
+    sem = T.sem
+    v, a, pe, sy = g.vector, g.scalar, g.tensor, g.sync
+    op = AluOpType
+    nv = [0]
+
+    def inc(ins):
+        ins.then_inc(sem["v"], 1)
+        nv[0] += 1
+
+    def flush():
+        v.wait_ge(sem["v"], nv[0])
+
+    if rank > 0:
+        sy.dma_start(T.vb[:, 0:128], T.bp[:]).then_inc(sem["ldb"], 16)
+    else:
+        sy.dma_start(T.sti[:], T.st[:]).then_inc(sem["ldb"], 16)
+    sy.dma_start(T.tabw[:, 0:FIRST], T.tab[:, 0:FIRST]).then_inc(sem["ldt"], 16)
+    if rank == N - 1:
+        for k in range(8):
+            a.dma_start(T.st8[16 * k:16 * k + 16, :], T.st[:]).then_inc(sem["lds"], 16)
+
+    if rank > 0:
+        inc(v.memset(T.vb[:, 128:132], 0))
+        flush()
+        v.wait_ge(sem["ldb"], 16)
+        inc(v.tensor_scalar(T.t1[:, 0:129], T.vb[:, 0:129], 15, None, op.bitwise_and))
+        inc(v.tensor_scalar(T.t2[:, 0:129], T.vb[:, 0:129], 7, 112, op.logical_shift_right, op.bitwise_and))
+        inc(v.tensor_scalar(T.u[:, 0:129], T.vb[:, 0:129], 2032, None, op.bitwise_and))
+        flush()
+        inc(v.tensor_tensor(T.lab[:, 0:129], T.t1[:, 0:129], T.t2[:, 0:129], op.add))
+        v.tensor_tensor(T.wout[:, 128:256], T.u[:, 1:129], T.u[:, 0:128], op.subtract).then_inc(sem["enc"], 1)
+        flush()
+        v.tensor_tensor(T.wout[:, 0:128], T.lab[:, 0:128], T.lab[:, 1:129], op.subtract).then_inc(sem["enc"], 1)
+        g.wait_ge(sem["enc"], 2)
+        total = fused(g, core, topo, walk, [T.wout[:]] * Q, [window(T, rank)] * Q,
+                      sem["map%d" % rank], sem["snt"])
+    else:
+        v.wait_ge(sem["ldb"], 16)
+        inc(v.tensor_scalar(T.t1[:, 0:16], T.sti[:], 15, None, op.bitwise_and))
+        inc(v.tensor_scalar(T.t2[:, 0:16], T.sti[:], 7, 112, op.logical_shift_right, op.bitwise_and))
+        inc(v.tensor_scalar(T.u[:, 0:16], T.sti[:], 2032, None, op.bitwise_and))
+        flush()
+        v.tensor_tensor(T.lst0[:, 1:32:2], T.t1[:, 0:16], T.t2[:, 0:16], op.add).then_inc(sem["enc"], 1)
+        v.tensor_scalar(T.lst0[:, 0:32:2], T.u[:, 0:16], -1.0, None, op.mult).then_inc(sem["enc"], 1)
+        g.wait_ge(sem["enc"], 2)
+        total = fused(g, core, topo, walk, [T.lst0[:, 8 * q:8 * q + 8] for q in range(Q)],
+                      [stile(T, 0, FIN, FIN + 8)] * Q, sem["st0"], sem["snt"])
+
+    sy.wait_ge(sem["snt"], total)
+    sy.dma_start(T.tabw[:, FIRST:], T.tab[:, FIRST:]).then_inc(sem["ldt"], 16)
+
+    if rank == N - 1:
+        v.wait_ge(sem["lds"], 128)
+        v.tensor_copy(T.offs[:], T.st8[:]).then_inc(sem["ofr"], 1)
+    else:
+        v.memset(T.e1[:], 1.0).then_inc(sem["g1"], 1)
+        g.iota(T.ji[:], [[-1, 8], [0, 16]], 8, 1).then_inc(sem["g3"], 1)
+        g.iota(T.pi[:], [[0, 8]], 0, 1).then_inc(sem["g4"], 1)
+        g.wait_ge(sem["g1"], 1)
+        g.affine_select(T.e2[:], T.e1[:], [[0, 8], [-8, 16]], op.is_ge, 0.0, 0, 1).then_inc(sem["g2"], 1)
+        g.wait_ge(sem["g2"], 1)
+        g.affine_select(T.e3[:], T.e2[:], [[0, 8], [8, 16]], op.is_ge, 0.0, 7, -1).then_inc(sem["g2"], 1)
+        v.wait_ge(sem["g3"], 1)
+        inc(v.tensor_scalar(T.ja[:], T.ji[:], 7, None, op.bitwise_and))
+        v.wait_ge(sem["g4"], 1)
+        inc(v.tensor_scalar(T.pa[:], T.pi[:], 15, None, op.bitwise_and))
+        flush()
+        inc(v.tensor_scalar(T.jm[:], T.ja[:], 0.0, None, op.is_equal))
+        inc(v.tensor_copy(T.coffs[:], T.pa[:]))
+        flush()
+        n_in = sum(len(bits(topo.mask(w, core))) for w in walk)
+        v.wait_ge(sem["lin"], n_in)
+        inc(v.tensor_scalar(T.hh[:], T.land[:, 1:32:2], 0.0625, -0.46875, op.mult, op.add))
+        inc(v.tensor_tensor(T.wsum[:], T.land[:, 1:32:2], T.land[:, 0:32:2], op.subtract))
+        flush()
+        inc(v.tensor_scalar(T.hf[:], T.hh[:], 2032.0, None, op.mult))
+        flush()
+        inc(v.tensor_tensor(T.sval[:], T.wsum[:], T.hf[:], op.add))
+        flush()
+        v.tensor_tensor(T.xsp[:], T.sval[:, 0:16].indirect(T.coffs[:, 0:8]), T.jm[:], op.mult).then_inc(sem["xr"], 1)
+        pe.wait_ge(sem["g2"], 2)
+        pe.wait_ge(sem["xr"], 1)
+        pe.matmul(T.R0[:, 0:128], T.e3[:], T.xsp[:], True, True).then_inc(sem["mm"], 1)
+        v.wait_ge(sem["mm"], 1)
+        v.tensor_copy(T.offs[:], T.R0[:, 0:128]).then_inc(sem["ofr"], 1)
+
+    W = 512
+
+    def part(k):
+        return T.yb[:, W * k:W * k + W], T.tabw[:, 0:16384].indirect(T.offs[:, 32 * k:32 * k + 32])
+
+    v.wait_ge(sem["ofr"], 1)
+    v.wait_ge(sem["ldt"], 32)
+    a.wait_ge(sem["ofr"], 1)
+    a.wait_ge(sem["ldt"], 32)
+    for k in (0, 1):
+        o, i = part(k)
+        v.tensor_copy(o, i).then_inc(sem["yd%d" % k], 1)
+    for k in (2, 3):
+        o, i = part(k)
+        a.activation(o, i, ActivationFunctionType.Copy).then_inc(sem["yd%d" % k], 1)
+    for k in (0, 2, 1):
+        sy.wait_ge(sem["yd%d" % k], 1)
+        sy.dma_start(T.y[:, W * k:W * k + W], T.yb[:, W * k:W * k + W]).then_inc(sem["sto"], 16)
+    a.wait_ge(sem["yd3"], 1)
+    a.dma_start(T.y[:, 3 * W:4 * W], T.yb[:, 3 * W:4 * W]).then_inc(sem["sto"], 16)
+    sy.wait_ge(sem["sto"], 64)

@@ -4,86 +4,76 @@ from concourse.mybir import AluOpType, ActivationFunctionType
 N = 9
 NCORES = 112
 Q = 4
-NB = 4
+NBL = 3
+NBF = 1
 STEPS = N - 1
 SW = 264
 FIN = 256
-FIRST = 2048
+FIRST = [2048, 5888, 5120, 4352, 3584, 2816, 2048, 2048, 2048]
+HOLD = N - 2
 
 SCRATCH = {
     "tabw": ("sbuf", [128, 16384], "bfloat16"),
     "yb": ("sbuf", [128, 2048], "bfloat16"),
-    "vb": ("sbuf", [128, 132], "int32"),
-    "u": ("sbuf", [128, 132], "int32"),
-    "t1": ("sbuf", [128, 132], "int32"),
-    "t2": ("sbuf", [128, 132], "int32"),
-    "lab": ("sbuf", [128, 132], "int32"),
     "wout": ("sbuf", [128, 256], "bfloat16"),
     "sti": ("sbuf", [128, 16], "int32"),
     "lst0": ("sbuf", [128, 32], "float32"),
     "st8": ("sbuf", [128, 128], "int32"),
     "land": ("sbuf", [128, 32], "float32"),
     "hh": ("sbuf", [128, 16], "int32"),
-    "hf": ("sbuf", [128, 16], "float32"),
-    "wsum": ("sbuf", [128, 16], "float32"),
-    "sval": ("sbuf", [128, 16], "float32"),
-    "xsp": ("sbuf", [128, 128], "float32"),
-    "e1": ("sbuf", [128, 128], "float32"),
-    "e2": ("sbuf", [128, 128], "float32"),
-    "e3": ("sbuf", [128, 128], "float32"),
-    "ji": ("sbuf", [128, 128], "int32"),
-    "ja": ("sbuf", [128, 128], "int32"),
-    "jm": ("sbuf", [128, 128], "float32"),
     "pi": ("sbuf", [128, 8], "int32"),
     "pa": ("sbuf", [128, 8], "int32"),
     "coffs": ("sbuf", [128, 8], "uint16"),
     "offs": ("sbuf", [128, 128], "uint16"),
-    "ones": ("sbuf", [128, 128], "bfloat16"),
-    "ident": ("sbuf", [128, 128], "bfloat16"),
-    "col": ("sbuf", [128, 128], "bfloat16"),
-    "lam": ("sbuf", [128, 128], "bfloat16"),
+    "ji": ("sbuf", [128, 128], "int32"),
+    "ja": ("sbuf", [128, 128], "int32"),
     "win": ("sbuf", [128, 256 * N], "bfloat16"),
     "S": ("sbuf", [128, SW * (STEPS + 1)], "float32"),
 }
-for _b in range(NB):
-    SCRATCH["O%d" % _b] = ("sbuf", [128, 128], "bfloat16")
-    SCRATCH["A%d" % _b] = ("sbuf", [128, 128], "bfloat16")
-    SCRATCH["M%d" % _b] = ("sbuf", [128, 128], "bfloat16")
+for _k in ("vb", "u", "t1", "t2", "lab"):
+    SCRATCH[_k] = ("sbuf", [128, 132], "int32")
+for _k in ("hf", "wsum", "sval"):
+    SCRATCH[_k] = ("sbuf", [128, 16], "float32")
+for _k in ("xsp", "e1", "e2", "e3", "jm"):
+    SCRATCH[_k] = ("sbuf", [128, 128], "float32")
+for _k in ("ones", "ident", "col", "lam"):
+    SCRATCH[_k] = ("sbuf", [128, 128], "bfloat16")
+for _b in range(NBL):
+    for _k in ("O", "A", "M"):
+        SCRATCH["%s%d" % (_k, _b)] = ("sbuf", [128, 128], "bfloat16")
     SCRATCH["P%d" % _b] = ("psum", [128, 1024], "bfloat16")
     SCRATCH["R%d" % _b] = ("psum", [128, 512], "float32")
 
-SEMAPHORES = (["ldb", "ldt", "lds", "v", "enc", "snt", "lin", "g1", "g2", "g3", "g4", "mm", "xr", "ofr", "sto",
+SEMAPHORES = (["ldb", "ldt", "lds", "v", "enc", "snt", "fwd", "lin", "g1", "g2", "g3", "g4", "mm", "xr", "ofr", "sto",
                "st0", "k1", "k2", "k3", "k4", "yd0", "yd1", "yd2", "yd3"]
               + ["map%d" % f for f in range(1, N)]
-              + ["%s%d" % (k, b) for k in ("O", "P", "A", "M", "R", "S", "F") for b in range(NB)])
+              + ["%s%d" % (k, b) for k in ("O", "P", "A", "M", "R", "S", "F") for b in range(NBL)])
 
 
 def walkers(T, topo):
     ranks = list(T.cores)
     used = [topo.chip(c) for c in ranks]
-    planes = []
-    seen = []
+    ok = {}
     for c in range(NCORES):
-        ch = topo.chip(c)
-        if ch in used or ch in seen or topo.die(c) != topo.die(ranks[0]):
-            continue
-        if not all(topo.may_write(c, r) for r in ranks):
-            continue
-        seen.append(ch)
+        if topo.chip(c) not in used and topo.die(c) == topo.die(ranks[0]) and all(topo.may_write(c, r) for r in ranks):
+            ok.setdefault(topo.chip(c), []).append(c)
+    planes, out, i = [], [], 0
+    for ch in sorted(ok):
         for pl in planes:
-            if topo.same_plane(topo.chip(pl[0]), ch):
-                pl.append(c)
+            if topo.same_plane(pl[0], ch):
+                pl.append(ch)
                 break
         else:
-            planes.append([c])
-    out = []
-    i = 0
+            planes.append([ch])
     while len(out) < Q:
-        for pl in planes:
-            if i < len(pl) and len(out) < Q:
-                out.append(pl[i])
+        out += [pl[i] for pl in planes if i < len(pl)]
         i += 1
-    return out
+    return [(ok[ch][0], ok[ch][1]) for ch in out[:Q]]
+
+
+def cols(q, k):
+    a = 2 * (NBL + NBF) * q
+    return (a, a + 2 * NBF) if k else (a + 2 * NBF, a + 2 * NBF + 2 * NBL)
 
 
 def stile(T, t, a, b, step=1):
@@ -123,17 +113,20 @@ def rank_program(g, core, T, topo):
     rank = T.rank_of(core)
     if rank is not None:
         run_rank(g, core, rank, T, topo, walk)
-    elif core in walk:
-        run_walker(g, core, walk.index(core), T, topo, walk)
+    for q, pair in enumerate(walk):
+        if core in pair:
+            run_walker(g, core, q, pair.index(core), T, topo, walk)
 
 
-def run_walker(g, core, q, T, topo, walk):
+def run_walker(g, core, q, follower, T, topo, walk):
     sem = T.sem
     v, a, pe = g.vector, g.scalar, g.tensor
     op = AluOpType
-    SS = [FIN + 7 - 2 * b for b in range(NB)]
-    SO = [FIN + 6 - 2 * b for b in range(NB)]
-    n_in = shares(T.cores[0], walk, topo)[1]
+    NB = NBF if follower else NBL
+    SS = [FIN + 2 * NB - 1 - 2 * b for b in range(NB)]
+    SO = [FIN + 2 * NB - 2 - 2 * b for b in range(NB)]
+    n_st = shares(T.cores[0], [w[0] for w in walk], topo)[1]
+    n_in = len(bits(topo.mask(walk[q][0], core))) if follower else n_st
 
     v.memset(T.ones[:], 1.0).then_inc(sem["k1"], 1)
     fl = dict(allow_small_or_imprecise_dtypes=True)
@@ -147,7 +140,7 @@ def run_walker(g, core, q, T, topo, walk):
                         op.is_equal).then_inc(sem["O%d" % b], 1)
 
     v.wait_ge(sem["k3"], 1)
-    v.wait_ge(sem["st0"], n_in)
+    v.wait_ge(sem["st0"], n_st)
     for b in range(NB):
         onehot(1, b)
     for t in range(1, STEPS + 1):
@@ -168,7 +161,7 @@ def run_walker(g, core, q, T, topo, walk):
                 onehot(t + 1, b)
 
     a.wait_ge(sem["k4"], 1)
-    a.wait_ge(sem["st0"], n_in)
+    a.wait_ge(sem["st0"], n_st)
     for t in range(1, STEPS + 1):
         for b in range(NB):
             if t > 1:
@@ -189,15 +182,31 @@ def run_walker(g, core, q, T, topo, walk):
     turn(0)
     for k in range(STEPS * NB):
         t, b = k // NB + 1, k % NB
-        if k + 1 < STEPS * NB:
+        if NB > 1 and k + 1 < STEPS * NB:
             turn(k + 1)
         f = N - t
         if b == 0:
             pe.wait_ge(sem["map%d" % f], n_in)
         pe.wait_ge(sem["M%d" % b], t)
         pe.matmul(T["R%d" % b][:, 0:256], T["M%d" % b][:], window(T, f), True, True).then_inc(sem["R%d" % b], 1)
+        if NB == 1 and k + 1 < STEPS:
+            turn(k + 1)
 
-    sent = 0
+    sent, passed = 0, 0
+
+    def forward(f):
+        dst = walk[q][1]
+        m = topo.mask(core, dst)
+        rid, pid, _ = topo.addr(dst)
+        g.wait_ge(sem["map%d" % f], n_in)
+        g.remote_dma(window(T, f), window(T, f), sem["map%d" % f], sem["fwd"], pid, rid, m)
+        return len(bits(m))
+
+    ahead = 3
+    if not follower:
+        for f in range(N - 1, N - 1 - ahead, -1):
+            passed += forward(f)
+    ca, cb = cols(q, follower)
     for t in range(1, STEPS + 1):
         for b in range(NB):
             g.wait_ge(sem["S%d" % b], t)
@@ -205,9 +214,14 @@ def run_walker(g, core, q, T, topo, walk):
         dst = T.cores[N - 1 - t]
         m = topo.mask(core, dst)
         rid, pid, _ = topo.addr(dst)
-        g.remote_dma(T.land[:, 8 * q:8 * q + 8], stile(T, t, FIN, FIN + 8), sem["lin"], sem["snt"], pid, rid, m)
+        g.remote_dma(T.land[:, ca:cb], stile(T, t, FIN, FIN + 2 * NB), sem["lin"], sem["snt"], pid, rid, m)
         sent += len(bits(m))
+        f = N - ahead - t
+        if not follower and f >= 1:
+            passed += forward(f)
     g.wait_ge(sem["snt"], sent)
+    if passed:
+        g.wait_ge(sem["fwd"], passed)
 
 
 def run_rank(g, core, rank, T, topo, walk):
@@ -223,11 +237,12 @@ def run_rank(g, core, rank, T, topo, walk):
     def flush():
         v.wait_ge(sem["v"], nv[0])
 
+    F = FIRST[rank]
     if rank > 0:
         sy.dma_start(T.vb[:, 0:128], T.bp[:]).then_inc(sem["ldb"], 16)
     else:
         sy.dma_start(T.sti[:], T.st[:]).then_inc(sem["ldb"], 16)
-    sy.dma_start(T.tabw[:, 0:FIRST], T.tab[:, 0:FIRST]).then_inc(sem["ldt"], 16)
+    sy.dma_start(T.tabw[:, 0:F], T.tab[:, 0:F]).then_inc(sem["ldt"], 16)
     if rank == N - 1:
         for k in range(8):
             a.dma_start(T.st8[16 * k:16 * k + 16, :], T.st[:]).then_inc(sem["lds"], 16)
@@ -245,7 +260,9 @@ def run_rank(g, core, rank, T, topo, walk):
         flush()
         v.tensor_tensor(T.wout[:, 0:128], T.lab[:, 0:128], T.lab[:, 1:129], op.subtract).then_inc(sem["enc"], 1)
         g.wait_ge(sem["enc"], 2)
-        total = fused(g, core, topo, walk, [T.wout[:]] * Q, [window(T, rank)] * Q,
+        if rank < HOLD:
+            g.wait_ge(sem["ldt"], 16)
+        total = fused(g, core, topo, [w[0] for w in walk], [T.wout[:]] * Q, [window(T, rank)] * Q,
                       sem["map%d" % rank], sem["snt"])
     else:
         v.wait_ge(sem["ldb"], 16)
@@ -256,11 +273,14 @@ def run_rank(g, core, rank, T, topo, walk):
         v.tensor_tensor(T.lst0[:, 1:32:2], T.t1[:, 0:16], T.t2[:, 0:16], op.add).then_inc(sem["enc"], 1)
         v.tensor_scalar(T.lst0[:, 0:32:2], T.u[:, 0:16], -1.0, None, op.mult).then_inc(sem["enc"], 1)
         g.wait_ge(sem["enc"], 2)
-        total = fused(g, core, topo, walk, [T.lst0[:, 8 * q:8 * q + 8] for q in range(Q)],
-                      [stile(T, 0, FIN, FIN + 8)] * Q, sem["st0"], sem["snt"])
+        total = 0
+        for k, nb in ((0, NBL), (1, NBF)):
+            at = [cols(q, k) for q in range(Q)]
+            total += fused(g, core, topo, [w[k] for w in walk], [T.lst0[:, x:y] for x, y in at],
+                           [stile(T, 0, FIN, FIN + 2 * nb)] * Q, sem["st0"], sem["snt"])
 
     sy.wait_ge(sem["snt"], total)
-    sy.dma_start(T.tabw[:, FIRST:], T.tab[:, FIRST:]).then_inc(sem["ldt"], 16)
+    sy.dma_start(T.tabw[:, F:], T.tab[:, F:]).then_inc(sem["ldt"], 16)
 
     if rank == N - 1:
         v.wait_ge(sem["lds"], 128)
@@ -281,7 +301,7 @@ def run_rank(g, core, rank, T, topo, walk):
         inc(v.tensor_scalar(T.jm[:], T.ja[:], 0.0, None, op.is_equal))
         inc(v.tensor_copy(T.coffs[:], T.pa[:]))
         flush()
-        n_in = sum(len(bits(topo.mask(w, core))) for w in walk)
+        n_in = sum(len(bits(topo.mask(w, core))) for pair in walk for w in pair)
         v.wait_ge(sem["lin"], n_in)
         inc(v.tensor_scalar(T.hh[:], T.land[:, 1:32:2], 0.0625, -0.46875, op.mult, op.add))
         inc(v.tensor_tensor(T.wsum[:], T.land[:, 1:32:2], T.land[:, 0:32:2], op.subtract))

@@ -1,53 +1,51 @@
 from concourse.bass import DstId, RemoteDMATransfer
-from concourse.mybir import AluOpType, ActivationFunctionType
+from concourse.mybir import AluOpType, ActivationFunctionType, AxisListType
 
 N = 9
 NCORES = 112
 Q = 4
-NBL = 3
-NBF = 1
+K = 4
 STEPS = N - 1
-SW = 264
-FIN = 256
-FIRST = [2048, 5888, 5120, 4352, 3584, 2816, 2048, 2048, 2048]
+FIRST = [2048, 4864, 4096, 3584, 3584, 2816, 2048, 1024, 512]
 HOLD = N - 2
+AHEAD = 4
 
 SCRATCH = {
     "tabw": ("sbuf", [128, 16384], "bfloat16"),
     "yb": ("sbuf", [128, 2048], "bfloat16"),
+    "vb": ("sbuf", [128, 128], "int32"),
+    "t1": ("sbuf", [128, 128], "int32"),
+    "t2": ("sbuf", [128, 128], "int32"),
+    "u0": ("sbuf", [128, 128], "int32"),
     "wout": ("sbuf", [128, 256], "bfloat16"),
-    "sti": ("sbuf", [128, 16], "int32"),
-    "lst0": ("sbuf", [128, 32], "float32"),
     "st8": ("sbuf", [128, 128], "int32"),
-    "land": ("sbuf", [128, 32], "float32"),
-    "hh": ("sbuf", [128, 16], "int32"),
-    "pi": ("sbuf", [128, 8], "int32"),
-    "pa": ("sbuf", [128, 8], "int32"),
-    "coffs": ("sbuf", [128, 8], "uint16"),
     "offs": ("sbuf", [128, 128], "uint16"),
+    "win": ("sbuf", [128, 256 * N], "bfloat16"),
+    "wins": ("sbuf", [128, 128], "int32"),
+    "woffs": ("sbuf", [128, 8], "uint16"),
+    "zo": ("sbuf", [128, 8 * STEPS], "uint16"),
     "ji": ("sbuf", [128, 128], "int32"),
     "ja": ("sbuf", [128, 128], "int32"),
-    "win": ("sbuf", [128, 256 * N], "bfloat16"),
-    "S": ("sbuf", [128, SW * (STEPS + 1)], "float32"),
+    "e3f": ("sbuf", [128, 128], "float32"),
+    "gs": ("sbuf", [128, 128], "float32"),
+    "labp": ("sbuf", [128, 1], "float32"),
+    "labc": ("sbuf", [128, 1], "float32"),
 }
-for _k in ("vb", "u", "t1", "t2", "lab"):
-    SCRATCH[_k] = ("sbuf", [128, 132], "int32")
-for _k in ("hf", "wsum", "sval"):
-    SCRATCH[_k] = ("sbuf", [128, 16], "float32")
-for _k in ("xsp", "e1", "e2", "e3", "jm"):
-    SCRATCH[_k] = ("sbuf", [128, 128], "float32")
-for _k in ("ones", "ident", "col", "lam"):
+for _k in ("pi", "hhp", "rp", "zi", "za", "zb", "zc"):
+    SCRATCH[_k] = ("sbuf", [128, 8], "int32")
+for _k in ("j1", "jm", "zl", "zj", "onesf", "us", "u8"):
+    SCRATCH[_k] = ("sbuf", [128, 8], "float32")
+for _k in ("c16", "fa", "fb", "ub"):
+    SCRATCH[_k] = ("sbuf", [128, 8], "bfloat16")
+for _k in ("ones", "ident", "e3b", "go0", "go1", "gl", "mask"):
     SCRATCH[_k] = ("sbuf", [128, 128], "bfloat16")
-for _b in range(NBL):
-    for _k in ("O", "A", "M"):
-        SCRATCH["%s%d" % (_k, _b)] = ("sbuf", [128, 128], "bfloat16")
-    SCRATCH["P%d" % _b] = ("psum", [128, 1024], "bfloat16")
-    SCRATCH["R%d" % _b] = ("psum", [128, 512], "float32")
+for _k in ("C", "XL", "Z", "CS", "ZS"):
+    SCRATCH[_k] = ("psum", [128, 512], "float32")
 
-SEMAPHORES = (["ldb", "ldt", "lds", "v", "enc", "snt", "fwd", "lin", "g1", "g2", "g3", "g4", "mm", "xr", "ofr", "sto",
-               "st0", "k1", "k2", "k3", "k4", "yd0", "yd1", "yd2", "yd3"]
-              + ["map%d" % f for f in range(1, N)]
-              + ["%s%d" % (k, b) for k in ("O", "P", "A", "M", "R", "S", "F") for b in range(NBL)])
+SEMAPHORES = (["ldb", "lda", "ldt", "lds", "v", "enc", "snt", "snl", "fwd", "lin", "ofr", "sto", "st0", "k1", "k2", "k3",
+               "k4", "k5", "k6", "ce", "yd0", "yd1", "yd2", "yd3",
+               "sgo", "sgl", "sc", "sxl", "su", "smk", "sz", "sof", "scs", "sus", "szs", "szo"]
+              + ["map%d" % f for f in range(1, N)])
 
 
 def walkers(T, topo):
@@ -55,10 +53,11 @@ def walkers(T, topo):
     used = [topo.chip(c) for c in ranks]
     ok = {}
     for c in range(NCORES):
-        if topo.chip(c) not in used and topo.die(c) == topo.die(ranks[0]) and all(topo.may_write(c, r) for r in ranks):
+        if topo.chip(c) not in used and all(topo.may_write(c, r) for r in ranks):
             ok.setdefault(topo.chip(c), []).append(c)
     planes, out, i = [], [], 0
     for ch in sorted(ok):
+        ok[ch].sort(key=lambda c: (topo.die(c) != topo.die(ranks[0]), c))
         for pl in planes:
             if topo.same_plane(pl[0], ch):
                 pl.append(ch)
@@ -68,20 +67,7 @@ def walkers(T, topo):
     while len(out) < Q:
         out += [pl[i] for pl in planes if i < len(pl)]
         i += 1
-    return [(ok[ch][0], ok[ch][1]) for ch in out[:Q]]
-
-
-def cols(q, k):
-    a = 2 * (NBL + NBF) * q
-    return (a, a + 2 * NBF) if k else (a + 2 * NBF, a + 2 * NBF + 2 * NBL)
-
-
-def stile(T, t, a, b, step=1):
-    return T.S[:, SW * t + a:SW * t + b:step]
-
-
-def window(T, f):
-    return T.win[:, 256 * f:256 * f + 256]
+    return [ok[ch][:K] for ch in out[:Q]]
 
 
 def bits(m):
@@ -97,137 +83,41 @@ def shares(src, dsts, topo):
     return [sum(e[i * n:(i + 1) * n]) for i in range(len(dsts))], n
 
 
+def dst_id(topo, d):
+    rid, pid, _ = topo.addr(d)
+    return DstId(rid=rid, pnc=pid)
+
+
 def fused(g, core, topo, dsts, srcs, outs, rsem, lsem):
     masks, n = shares(core, dsts, topo)
-    tr = []
-    for d, m, s, o in zip(dsts, masks, srcs, outs):
-        rid, pid, _ = topo.addr(d)
-        tr.append(RemoteDMATransfer(dst_ids=[DstId(rid=rid, pnc=pid)], dma_engine_mask=m, remote_sem=rsem,
-                                    srcs=[s], dsts=[o], alu_op=0))
+    tr = [RemoteDMATransfer(dst_ids=[dst_id(topo, d)], dma_engine_mask=m, remote_sem=rsem, srcs=[s], dsts=[o], alu_op=0)
+          for d, m, s, o in zip(dsts, masks, srcs, outs)]
     g.remote_dma_fused(tr, local_sem=lsem)
     return n * len(dsts)
 
 
+def window(T, f):
+    return T.win[:, 256 * f:256 * f + 256] if f > 1 else T.wins[:]
+
+
 def rank_program(g, core, T, topo):
-    walk = walkers(T, topo)
+    teams = walkers(T, topo)
     rank = T.rank_of(core)
     if rank is not None:
-        run_rank(g, core, rank, T, topo, walk)
-    for q, pair in enumerate(walk):
-        if core in pair:
-            run_walker(g, core, q, pair.index(core), T, topo, walk)
+        run_rank(g, core, rank, T, topo, teams)
+    for q, team in enumerate(teams):
+        if core in team:
+            run_walker(g, core, q, team.index(core), T, topo, teams)
 
 
-def run_walker(g, core, q, follower, T, topo, walk):
+def run_walker(g, core, q, k, T, topo, teams):
     sem = T.sem
-    v, a, pe = g.vector, g.scalar, g.tensor
+    v, pe = g.vector, g.tensor
     op = AluOpType
-    NB = NBF if follower else NBL
-    SS = [FIN + 2 * NB - 1 - 2 * b for b in range(NB)]
-    SO = [FIN + 2 * NB - 2 - 2 * b for b in range(NB)]
-    n_st = shares(T.cores[0], [w[0] for w in walk], topo)[1]
-    n_in = len(bits(topo.mask(walk[q][0], core))) if follower else n_st
-
-    v.memset(T.ones[:], 1.0).then_inc(sem["k1"], 1)
-    fl = dict(allow_small_or_imprecise_dtypes=True)
-    g.iota(T.lam[:], [[1, 16], [16, 8]], 0, 0, **fl).then_inc(sem["k3"], 1)
-    g.iota(T.col[:], [[1, 128]], 0, 0, **fl).then_inc(sem["k4"], 1)
-    g.wait_ge(sem["k1"], 1)
-    g.affine_select(T.ident[:], T.ones[:], [[-1, 128]], op.is_equal, 0.0, 0, 1).then_inc(sem["k2"], 1)
-
-    def onehot(t, b):
-        v.tensor_scalar(T["O%d" % b][:], T.lam[:], stile(T, t - 1, SS[b], SS[b] + 1), None,
-                        op.is_equal).then_inc(sem["O%d" % b], 1)
-
-    v.wait_ge(sem["k3"], 1)
-    v.wait_ge(sem["st0"], n_st)
-    for b in range(NB):
-        onehot(1, b)
-    for t in range(1, STEPS + 1):
-        for b in range(NB):
-            A, R = T["A%d" % b], T["R%d" % b]
-            v.wait_ge(sem["A%d" % b], t)
-            v.wait_ge(sem["R%d" % b], t)
-            if b > 0:
-                v.wait_ge(sem["S%d" % (b - 1)], t)
-            v.tensor_tensor_scan(stile(T, t, SS[b] - 254, SS[b] + 1, 2), A[:], R[:, 0:128], 0.0, op.mult,
-                                 op.add).then_inc(sem["S%d" % b], 1)
-            if b > 0:
-                v.wait_ge(sem["F%d" % (b - 1)], t)
-            v.tensor_tensor_scan(stile(T, t, SO[b] - 254, SO[b] + 1, 2), A[:], R[:, 128:256], 0.0, op.mult,
-                                 op.add).then_inc(sem["F%d" % b], 1)
-            if t < STEPS:
-                v.wait_ge(sem["S%d" % b], t)
-                onehot(t + 1, b)
-
-    a.wait_ge(sem["k4"], 1)
-    a.wait_ge(sem["st0"], n_st)
-    for t in range(1, STEPS + 1):
-        for b in range(NB):
-            if t > 1:
-                a.wait_ge(sem["S%d" % b], t - 1)
-                a.wait_ge(sem["F%d" % b], t - 1)
-            a.activation(T["A%d" % b][:], T.col[:], ActivationFunctionType.Sign,
-                         bias=stile(T, t - 1, SO[b], SO[b] + 1), scale=16.0).then_inc(sem["A%d" % b], 1)
-            a.wait_ge(sem["P%d" % b], t)
-            a.activation(T["M%d" % b][:], T["P%d" % b][:, 0:128],
-                         ActivationFunctionType.Copy).then_inc(sem["M%d" % b], 1)
-
-    def turn(k):
-        t, b = k // NB + 1, k % NB
-        pe.wait_ge(sem["O%d" % b], t)
-        pe.transpose(T["P%d" % b][:, 0:128], T["O%d" % b][:], T.ident[:]).then_inc(sem["P%d" % b], 1)
-
-    pe.wait_ge(sem["k2"], 1)
-    turn(0)
-    for k in range(STEPS * NB):
-        t, b = k // NB + 1, k % NB
-        if NB > 1 and k + 1 < STEPS * NB:
-            turn(k + 1)
-        f = N - t
-        if b == 0:
-            pe.wait_ge(sem["map%d" % f], n_in)
-        pe.wait_ge(sem["M%d" % b], t)
-        pe.matmul(T["R%d" % b][:, 0:256], T["M%d" % b][:], window(T, f), True, True).then_inc(sem["R%d" % b], 1)
-        if NB == 1 and k + 1 < STEPS:
-            turn(k + 1)
-
-    sent, passed = 0, 0
-
-    def forward(f):
-        dst = walk[q][1]
-        m = topo.mask(core, dst)
-        rid, pid, _ = topo.addr(dst)
-        g.wait_ge(sem["map%d" % f], n_in)
-        g.remote_dma(window(T, f), window(T, f), sem["map%d" % f], sem["fwd"], pid, rid, m)
-        return len(bits(m))
-
-    ahead = 3
-    if not follower:
-        for f in range(N - 1, N - 1 - ahead, -1):
-            passed += forward(f)
-    ca, cb = cols(q, follower)
-    for t in range(1, STEPS + 1):
-        for b in range(NB):
-            g.wait_ge(sem["S%d" % b], t)
-            g.wait_ge(sem["F%d" % b], t)
-        dst = T.cores[N - 1 - t]
-        m = topo.mask(core, dst)
-        rid, pid, _ = topo.addr(dst)
-        g.remote_dma(T.land[:, ca:cb], stile(T, t, FIN, FIN + 2 * NB), sem["lin"], sem["snt"], pid, rid, m)
-        sent += len(bits(m))
-        f = N - ahead - t
-        if not follower and f >= 1:
-            passed += forward(f)
-    g.wait_ge(sem["snt"], sent)
-    if passed:
-        g.wait_ge(sem["fwd"], passed)
-
-
-def run_rank(g, core, rank, T, topo, walk):
-    sem = T.sem
-    v, a, pe, sy = g.vector, g.scalar, g.tensor, g.sync
-    op = AluOpType
+    team = teams[q]
+    w = K * q + k
+    n_st = shares(T.cores[q], team, topo)[1]
+    n_in = len(bits(topo.mask(team[0], core))) if k else shares(T.cores[1], [t[0] for t in teams], topo)[1]
     nv = [0]
 
     def inc(ins):
@@ -237,104 +127,214 @@ def run_rank(g, core, rank, T, topo, walk):
     def flush():
         v.wait_ge(sem["v"], nv[0])
 
+    v.memset(T.ones[:], 1.0).then_inc(sem["k1"], 1)
+    v.memset(T.onesf[:], 1.0).then_inc(sem["k1"], 1)
+    v.memset(T.c16[:], 16.0).then_inc(sem["ce"], 1)
+    g.iota(T.pi[:], [[0, 8]], 0, 1).then_inc(sem["k2"], 1)
+    g.iota(T.ji[:], [[-1, 128]], 128, 1).then_inc(sem["k3"], 1)
+    g.wait_ge(sem["k1"], 2)
+    g.affine_select(T.j1[:], T.onesf[:], [[-16, 8]], op.is_ge, 0.0, 0, 1).then_inc(sem["k4"], 1)
+    g.wait_ge(sem["k4"], 1)
+    g.affine_select(T.jm[:], T.j1[:], [[16, 8]], op.is_ge, 0.0, 15, -1).then_inc(sem["k5"], 1)
+    g.affine_select(T.ident[:], T.ones[:], [[-1, 128]], op.is_equal, 0.0, 0, 1).then_inc(sem["k6"], 1)
+    v.wait_ge(sem["k2"], 1)
+    inc(v.tensor_scalar(T.hhp[:], T.pi[:], 7, None, op.bitwise_and))
+    inc(v.tensor_scalar(T.rp[:], T.pi[:], 3, None, op.logical_shift_right))
+    v.wait_ge(sem["k3"], 1)
+    inc(v.tensor_scalar(T.ja[:], T.ji[:], 15, None, op.bitwise_and))
+    flush()
+    v.tensor_scalar(T.fa[:], T.hhp[:], 2048.0, None, op.mult).then_inc(sem["ce"], 1)
+    inc(v.tensor_copy(T.fb[:], T.rp[:]))
+    v.tensor_scalar(T.e3b[:], T.ja[:], 0.0, None, op.is_equal).then_inc(sem["ce"], 1)
+    v.tensor_scalar(T.e3f[:], T.ja[:], 0.0, None, op.is_equal).then_inc(sem["ce"], 1)
+    flush()
+    inc(v.tensor_scalar(T.labp[:], T.hhp[:, 0:1], 16.0, T.fb[:, 0:1], op.mult, op.add))
+
+    v.wait_ge(sem["st0"], n_st)
+    inc(v.tensor_scalar(T.za[:], T.zi[:], 15, None, op.bitwise_and))
+    inc(v.tensor_scalar(T.zb[:], T.zi[:], 7, 112, op.logical_shift_right, op.bitwise_and))
+    inc(v.tensor_scalar(T.zc[:], T.zi[:], 4, 127, op.logical_shift_right, op.bitwise_and))
+    flush()
+    inc(v.tensor_tensor(T.zl[:], T.za[:], T.zb[:], op.add))
+    v.tensor_copy(T.woffs[:], T.zc[:]).then_inc(sem["sof"], 1)
+    v.wait_ge(sem["k5"], 1)
+    flush()
+    inc(v.tensor_tensor(T.zj[:], T.zl[:], T.jm[:], op.mult))
+    flush()
+    inc(v.tensor_reduce(T.labc[:], T.zj[:], AxisListType.X, op.add))
+    v.wait_ge(sem["k6"], 1)
+    flush()
+    v.tensor_scalar(T.gl[:], T.ident[:], T.labc[:], None, op.mult).then_inc(sem["sgl"], 1)
+
+    def next_mask(t):
+        v.wait_ge(sem["sxl"], t)
+        v.tensor_scalar(T.mask[:], T.XL[:, 0:128], T.labp[:], None, op.is_equal).then_inc(sem["smk"], 1)
+
+    def state_spread(t):
+        if t > 0:
+            v.wait_ge(sem["scs"], t)
+            v.tensor_tensor(T.us[:], T.CS[:, 0:8], T.jm[:], op.mult).then_inc(sem["sus"], 1)
+
+    def offsets_out(t, bank, s, n):
+        if t > 0:
+            v.wait_ge(sem[s], n)
+            v.tensor_copy(T.zo[:, 8 * t - 8:8 * t], bank[:, 0:8]).then_inc(sem["szo"], 1)
+
+    next_mask(1)
+    for t in range(1, STEPS + 1):
+        f = N - t
+        v.wait_ge(sem["map%d" % f], n_in)
+        v.wait_ge(sem["sof"], t)
+        v.wait_ge(sem["smk"], t)
+        if f > 1:
+            a = 256 * f
+            go = T["go%d" % (t % 2)]
+            v.tensor_tensor(go[:], T.win[:, a:a + 128].indirect(T.woffs[:, 0:8]), T.mask[:],
+                            op.mult).then_inc(sem["sgo"], 1)
+            v.tensor_tensor(T.gl[:], T.win[:, a + 128:a + 256].indirect(T.woffs[:, 0:8]), T.mask[:],
+                            op.mult).then_inc(sem["sgl"], 1)
+            state_spread(t - 1)
+            v.wait_ge(sem["sc"], t)
+            v.tensor_tensor(T.ub[:], T.C[:, 0:8], T.jm[:], op.mult).then_inc(sem["su"], 1)
+            next_mask(t + 1)
+            v.wait_ge(sem["sz"], t)
+            v.tensor_copy(T.woffs[:], T.Z[:, 0:8]).then_inc(sem["sof"], 1)
+        else:
+            v.tensor_tensor(T.gs[:], T.wins[:, 0:128].indirect(T.woffs[:, 0:8]), T.mask[:],
+                            op.mult).then_inc(sem["sgo"], 1)
+            state_spread(t - 1)
+            v.wait_ge(sem["sc"], t)
+            v.tensor_tensor(T.u8[:], T.C[:, 0:8], T.jm[:], op.mult).then_inc(sem["sus"], 1)
+        offsets_out(t - 1, T.ZS, "szs", t - 1)
+    offsets_out(STEPS, T.Z, "sz", STEPS)
+
+    pe.wait_ge(sem["k1"], 2)
+    pe.wait_ge(sem["ce"], 4)
+    pe.wait_ge(sem["v"], nv[0])
+    pe.wait_ge(sem["sgl"], 1)
+    pe.matmul(T.XL[:, 0:128], T.ones[:], T.gl[:], True, True).then_inc(sem["sxl"], 1)
+    for t in range(1, STEPS):
+        go = T["go%d" % (t % 2)]
+        pe.wait_ge(sem["sgo"], t)
+        pe.matmul(T.C[:, 0:8], go[:], T.ones[:, 0:8], True, True).then_inc(sem["sc"], 1)
+        pe.wait_ge(sem["sgl"], t + 1)
+        pe.matmul(T.XL[:, 0:128], T.ones[:], T.gl[:], True, True).then_inc(sem["sxl"], 1)
+        pe.wait_ge(sem["su"], t)
+        pe.matmul(T.Z[:, 0:8], T.e3b[:], T.ub[:], True, True).then_inc(sem["sz"], 1)
+        if t > 1:
+            pe.wait_ge(sem["sus"], t - 1)
+            if t > 2:
+                pe.wait_ge(sem["szo"], t - 2)
+            pe.matmul(T.ZS[:, 0:8], T.e3f[:], T.us[:], True, True).then_inc(sem["szs"], 1)
+        pe.wait_ge(sem["smk"], t + 1)
+        pe.matmul(T.CS[:, 0:8], go[:], T.c16[:], True, False)
+        pe.matmul(T.CS[:, 0:8], T.mask[:], T.fa[:], False, False)
+        pe.matmul(T.CS[:, 0:8], T.mask[:], T.fb[:], False, True).then_inc(sem["scs"], 1)
+    pe.wait_ge(sem["sgo"], STEPS)
+    pe.matmul(T.C[:, 0:8], T.gs[:], T.onesf[:], True, True).then_inc(sem["sc"], 1)
+    pe.wait_ge(sem["sus"], STEPS - 1)
+    pe.wait_ge(sem["szo"], STEPS - 2)
+    pe.matmul(T.ZS[:, 0:8], T.e3f[:], T.us[:], True, True).then_inc(sem["szs"], 1)
+    pe.wait_ge(sem["sus"], STEPS)
+    pe.matmul(T.Z[:, 0:8], T.e3f[:], T.u8[:], True, True).then_inc(sem["sz"], 1)
+
+    sent, passed = 0, 0
+
+    def forward(f):
+        g.wait_ge(sem["map%d" % f], n_in)
+        m = topo.mask(core, team[1])
+        g.remote_dma_fused([RemoteDMATransfer(dst_ids=[dst_id(topo, d) for d in team[1:]], dma_engine_mask=m,
+                                              remote_sem=sem["map%d" % f], srcs=[window(T, f)],
+                                              dsts=[window(T, f)] * (K - 1), alu_op=0)], local_sem=sem["fwd"])
+        return len(bits(m))
+
+    if k == 0:
+        for f in range(N - 1, N - 1 - AHEAD, -1):
+            passed += forward(f)
+    for t in range(1, STEPS + 1):
+        g.wait_ge(sem["szo"], t)
+        dst = T.cores[N - 1 - t]
+        m = topo.mask(core, dst)
+        rid, pid, _ = topo.addr(dst)
+        g.remote_dma(T.offs[:, 8 * w:8 * w + 8], T.zo[:, 8 * t - 8:8 * t], sem["lin"], sem["snt"], pid, rid, m)
+        sent += len(bits(m))
+        f = N - AHEAD - t
+        if k == 0 and f >= 1:
+            passed += forward(f)
+    g.wait_ge(sem["snt"], sent)
+    if passed:
+        g.wait_ge(sem["fwd"], passed)
+
+
+def run_rank(g, core, rank, T, topo, teams):
+    sem = T.sem
+    v, a, sy = g.vector, g.scalar, g.sync
+    op = AluOpType
+    lister = rank < Q
+
     F = FIRST[rank]
+    if lister or rank == N - 1:
+        for i in range(8):
+            e = sy if lister and i % 2 else a
+            e.dma_start(T.st8[16 * i:16 * i + 16, :], T.st[:]).then_inc(sem["lds"], 16)
     if rank > 0:
-        sy.dma_start(T.vb[:, 0:128], T.bp[:]).then_inc(sem["ldb"], 16)
-    else:
-        sy.dma_start(T.sti[:], T.st[:]).then_inc(sem["ldb"], 16)
-    sy.dma_start(T.tabw[:, 0:F], T.tab[:, 0:F]).then_inc(sem["ldt"], 16)
-    if rank == N - 1:
-        for k in range(8):
-            a.dma_start(T.st8[16 * k:16 * k + 16, :], T.st[:]).then_inc(sem["lds"], 16)
+        sy.dma_start(T.vb[:], T.bp[:]).then_inc(sem["ldb"], 16)
+    if lister:
+        g.wait_ge(sem["lds"], 128)
+        n = fused(g, core, topo, teams[rank],
+                  [T.st8[:, 8 * w:8 * w + 8] for w in range(K * rank, K * rank + K)], [T.zi[:]] * K,
+                  sem["st0"], sem["snl"])
+        sy.wait_ge(sem["snl"], n)
+    sy.dma_start(T.tabw[:, 0:F], T.tab[:, 0:F]).then_inc(sem["lda"], 16)
 
     if rank > 0:
-        inc(v.memset(T.vb[:, 128:132], 0))
-        flush()
-        v.wait_ge(sem["ldb"], 16)
-        inc(v.tensor_scalar(T.t1[:, 0:129], T.vb[:, 0:129], 15, None, op.bitwise_and))
-        inc(v.tensor_scalar(T.t2[:, 0:129], T.vb[:, 0:129], 7, 112, op.logical_shift_right, op.bitwise_and))
-        inc(v.tensor_scalar(T.u[:, 0:129], T.vb[:, 0:129], 2032, None, op.bitwise_and))
-        flush()
-        inc(v.tensor_tensor(T.lab[:, 0:129], T.t1[:, 0:129], T.t2[:, 0:129], op.add))
-        v.tensor_tensor(T.wout[:, 128:256], T.u[:, 1:129], T.u[:, 0:128], op.subtract).then_inc(sem["enc"], 1)
-        flush()
-        v.tensor_tensor(T.wout[:, 0:128], T.lab[:, 0:128], T.lab[:, 1:129], op.subtract).then_inc(sem["enc"], 1)
-        g.wait_ge(sem["enc"], 2)
+        if rank > 1:
+            v.wait_ge(sem["ldb"], 16)
+            v.tensor_scalar(T.t1[:], T.vb[:], 15, None, op.bitwise_and).then_inc(sem["v"], 1)
+            v.tensor_scalar(T.t2[:], T.vb[:], 7, 112, op.logical_shift_right, op.bitwise_and).then_inc(sem["v"], 1)
+            v.tensor_scalar(T.u0[:], T.vb[:], 4, 127, op.logical_shift_right, op.bitwise_and).then_inc(sem["v"], 1)
+            v.wait_ge(sem["v"], 2)
+            v.tensor_tensor(T.wout[:, 128:256], T.t1[:], T.t2[:], op.add).then_inc(sem["enc"], 1)
+            v.wait_ge(sem["v"], 3)
+            v.tensor_copy(T.wout[:, 0:128], T.u0[:]).then_inc(sem["enc"], 1)
+            g.wait_ge(sem["enc"], 2)
+        else:
+            g.wait_ge(sem["ldb"], 16)
         if rank < HOLD:
-            g.wait_ge(sem["ldt"], 16)
-        total = fused(g, core, topo, [w[0] for w in walk], [T.wout[:]] * Q, [window(T, rank)] * Q,
-                      sem["map%d" % rank], sem["snt"])
-    else:
-        v.wait_ge(sem["ldb"], 16)
-        inc(v.tensor_scalar(T.t1[:, 0:16], T.sti[:], 15, None, op.bitwise_and))
-        inc(v.tensor_scalar(T.t2[:, 0:16], T.sti[:], 7, 112, op.logical_shift_right, op.bitwise_and))
-        inc(v.tensor_scalar(T.u[:, 0:16], T.sti[:], 2032, None, op.bitwise_and))
-        flush()
-        v.tensor_tensor(T.lst0[:, 1:32:2], T.t1[:, 0:16], T.t2[:, 0:16], op.add).then_inc(sem["enc"], 1)
-        v.tensor_scalar(T.lst0[:, 0:32:2], T.u[:, 0:16], -1.0, None, op.mult).then_inc(sem["enc"], 1)
-        g.wait_ge(sem["enc"], 2)
-        total = 0
-        for k, nb in ((0, NBL), (1, NBF)):
-            at = [cols(q, k) for q in range(Q)]
-            total += fused(g, core, topo, [w[k] for w in walk], [T.lst0[:, x:y] for x, y in at],
-                           [stile(T, 0, FIN, FIN + 2 * nb)] * Q, sem["st0"], sem["snt"])
+            g.wait_ge(sem["lda"], 16)
+        n = fused(g, core, topo, [t[0] for t in teams], [T.wout[:] if rank > 1 else T.vb[:]] * Q,
+                  [window(T, rank)] * Q, sem["map%d" % rank], sem["snt"])
+        sy.wait_ge(sem["snt"], n)
 
-    sy.wait_ge(sem["snt"], total)
     sy.dma_start(T.tabw[:, F:], T.tab[:, F:]).then_inc(sem["ldt"], 16)
 
     if rank == N - 1:
         v.wait_ge(sem["lds"], 128)
         v.tensor_copy(T.offs[:], T.st8[:]).then_inc(sem["ofr"], 1)
+        got, n_in = sem["ofr"], 1
     else:
-        v.memset(T.e1[:], 1.0).then_inc(sem["g1"], 1)
-        g.iota(T.ji[:], [[-1, 8], [0, 16]], 8, 1).then_inc(sem["g3"], 1)
-        g.iota(T.pi[:], [[0, 8]], 0, 1).then_inc(sem["g4"], 1)
-        g.wait_ge(sem["g1"], 1)
-        g.affine_select(T.e2[:], T.e1[:], [[0, 8], [-8, 16]], op.is_ge, 0.0, 0, 1).then_inc(sem["g2"], 1)
-        g.wait_ge(sem["g2"], 1)
-        g.affine_select(T.e3[:], T.e2[:], [[0, 8], [8, 16]], op.is_ge, 0.0, 7, -1).then_inc(sem["g2"], 1)
-        v.wait_ge(sem["g3"], 1)
-        inc(v.tensor_scalar(T.ja[:], T.ji[:], 7, None, op.bitwise_and))
-        v.wait_ge(sem["g4"], 1)
-        inc(v.tensor_scalar(T.pa[:], T.pi[:], 15, None, op.bitwise_and))
-        flush()
-        inc(v.tensor_scalar(T.jm[:], T.ja[:], 0.0, None, op.is_equal))
-        inc(v.tensor_copy(T.coffs[:], T.pa[:]))
-        flush()
-        n_in = sum(len(bits(topo.mask(w, core))) for pair in walk for w in pair)
-        v.wait_ge(sem["lin"], n_in)
-        inc(v.tensor_scalar(T.hh[:], T.land[:, 1:32:2], 0.0625, -0.46875, op.mult, op.add))
-        inc(v.tensor_tensor(T.wsum[:], T.land[:, 1:32:2], T.land[:, 0:32:2], op.subtract))
-        flush()
-        inc(v.tensor_scalar(T.hf[:], T.hh[:], 2032.0, None, op.mult))
-        flush()
-        inc(v.tensor_tensor(T.sval[:], T.wsum[:], T.hf[:], op.add))
-        flush()
-        v.tensor_tensor(T.xsp[:], T.sval[:, 0:16].indirect(T.coffs[:, 0:8]), T.jm[:], op.mult).then_inc(sem["xr"], 1)
-        pe.wait_ge(sem["g2"], 2)
-        pe.wait_ge(sem["xr"], 1)
-        pe.matmul(T.R0[:, 0:128], T.e3[:], T.xsp[:], True, True).then_inc(sem["mm"], 1)
-        v.wait_ge(sem["mm"], 1)
-        v.tensor_copy(T.offs[:], T.R0[:, 0:128]).then_inc(sem["ofr"], 1)
+        got, n_in = sem["lin"], sum(len(bits(topo.mask(w, core))) for team in teams for w in team)
 
-    W = 512
+    H = 1024
+    cut = [(0, 384), (384, H), (H, H + 384), (H + 384, 2 * H)]
 
     def part(k):
-        return T.yb[:, W * k:W * k + W], T.tabw[:, 0:16384].indirect(T.offs[:, 32 * k:32 * k + 32])
+        x, y = cut[k]
+        return T.yb[:, x:y], T.tabw[:, 0:16384].indirect(T.offs[:, x // 16:y // 16])
 
-    v.wait_ge(sem["ofr"], 1)
-    v.wait_ge(sem["ldt"], 32)
-    a.wait_ge(sem["ofr"], 1)
-    a.wait_ge(sem["ldt"], 32)
+    for e in (v, a):
+        e.wait_ge(sem["lda"], 16)
+        e.wait_ge(sem["ldt"], 16)
+        e.wait_ge(got, n_in)
     for k in (0, 1):
         o, i = part(k)
         v.tensor_copy(o, i).then_inc(sem["yd%d" % k], 1)
     for k in (2, 3):
         o, i = part(k)
         a.activation(o, i, ActivationFunctionType.Copy).then_inc(sem["yd%d" % k], 1)
-    for k in (0, 2, 1):
-        sy.wait_ge(sem["yd%d" % k], 1)
-        sy.dma_start(T.y[:, W * k:W * k + W], T.yb[:, W * k:W * k + W]).then_inc(sem["sto"], 16)
-    a.wait_ge(sem["yd3"], 1)
-    a.dma_start(T.y[:, 3 * W:4 * W], T.yb[:, 3 * W:4 * W]).then_inc(sem["sto"], 16)
+    for k in (0, 2, 1, 3):
+        e = a if k == 3 else sy
+        x, y = cut[k]
+        e.wait_ge(sem["yd%d" % k], 1)
+        e.dma_start(T.y[:, x:y], T.yb[:, x:y]).then_inc(sem["sto"], 16)
     sy.wait_ge(sem["sto"], 64)

@@ -1,51 +1,57 @@
 from concourse.bass import DstId, RemoteDMATransfer
-from concourse.mybir import AluOpType, ActivationFunctionType, AxisListType
+from concourse.mybir import AluOpType, ActivationFunctionType
 
 N = 9
 NCORES = 112
 Q = 4
 K = 4
 STEPS = N - 1
-FIRST = [2048, 4864, 4096, 3584, 3584, 2816, 2048, 1024, 512]
+HALF = range(1, N - 2)
+FIRST = [2048, 4096, 3584, 3072, 2816, 2048, 1536, 1024, 512]
+SECOND = 1024
 HOLD = N - 2
-AHEAD = 4
+AHEAD = 7
+JUMP = 16384.0
+DROP = -1048576.0
+PIECES = [320, 384, 320]
 
 SCRATCH = {
     "tabw": ("sbuf", [128, 16384], "bfloat16"),
     "yb": ("sbuf", [128, 2048], "bfloat16"),
-    "vb": ("sbuf", [128, 128], "int32"),
-    "t1": ("sbuf", [128, 128], "int32"),
-    "t2": ("sbuf", [128, 128], "int32"),
-    "u0": ("sbuf", [128, 128], "int32"),
+    "vb": ("sbuf", [128, 256], "int32"),
+    "tx": ("sbuf", [128, 256], "int32"),
+    "ty": ("sbuf", [128, 256], "int32"),
+    "tz": ("sbuf", [128, 128], "int32"),
     "wout": ("sbuf", [128, 256], "bfloat16"),
+    "wu": ("sbuf", [128, 128], "uint16"),
     "st8": ("sbuf", [128, 128], "int32"),
     "offs": ("sbuf", [128, 128], "uint16"),
-    "win": ("sbuf", [128, 256 * N], "bfloat16"),
-    "wins": ("sbuf", [128, 128], "int32"),
+    "win": ("sbuf", [128, 256 * (N - 1)], "bfloat16"),
+    "winu": ("sbuf", [128, 128], "uint16"),
     "woffs": ("sbuf", [128, 8], "uint16"),
+    "nof": ("sbuf", [128, 8], "uint16"),
     "zo": ("sbuf", [128, 8 * STEPS], "uint16"),
-    "ji": ("sbuf", [128, 128], "int32"),
-    "ja": ("sbuf", [128, 128], "int32"),
-    "e3f": ("sbuf", [128, 128], "float32"),
-    "gs": ("sbuf", [128, 128], "float32"),
-    "labp": ("sbuf", [128, 1], "float32"),
-    "labc": ("sbuf", [128, 1], "float32"),
+    "cols": ("sbuf", [128, 5], "float32"),
 }
-for _k in ("pi", "hhp", "rp", "zi", "za", "zb", "zc"):
+for _k in ("ji", "ja", "m32", "c8", "a8"):
+    SCRATCH[_k] = ("sbuf", [128, 128], "int32")
+for _k in ("e3f", "gs", "onesf", "da", "db", "d0", "xs"):
+    SCRATCH[_k] = ("sbuf", [128, 128], "float32")
+for _k in ("pi", "ni", "hw", "rw", "hh", "rh", "pa", "zi", "za", "zb", "zc"):
     SCRATCH[_k] = ("sbuf", [128, 8], "int32")
-for _k in ("j1", "jm", "zl", "zj", "onesf", "us", "u8"):
+for _k in ("j1", "jm", "zl", "us"):
     SCRATCH[_k] = ("sbuf", [128, 8], "float32")
-for _k in ("c16", "fa", "fb", "ub"):
+for _k in ("c16w", "faw", "fbw", "c16h", "fah", "fbh"):
     SCRATCH[_k] = ("sbuf", [128, 8], "bfloat16")
-for _k in ("ones", "ident", "e3b", "go0", "go1", "gl", "mask"):
+for _k in ("ones", "onest", "onesb", "w64", "ident", "go0", "go1", "gl", "mask"):
     SCRATCH[_k] = ("sbuf", [128, 128], "bfloat16")
-for _k in ("C", "XL", "Z", "CS", "ZS"):
+for _k in ("CB", "XL", "CS", "ZS"):
     SCRATCH[_k] = ("psum", [128, 512], "float32")
 
 SEMAPHORES = (["ldb", "lda", "ldt", "lds", "v", "enc", "snt", "snl", "fwd", "lin", "ofr", "sto", "st0", "k1", "k2", "k3",
-               "k4", "k5", "k6", "ce", "yd0", "yd1", "yd2", "yd3",
-               "sgo", "sgl", "sc", "sxl", "su", "smk", "sz", "sof", "scs", "sus", "szs", "szo"]
-              + ["map%d" % f for f in range(1, N)])
+               "k4", "k5", "k6", "k7", "cv", "ca",
+               "sgo", "sgl", "sc", "sxl", "ssc", "smk", "sof", "scs", "sus", "szs", "szo"]
+              + ["yd%d" % i for i in range(2 * len(PIECES))] + ["map%d" % f for f in range(1, N)])
 
 
 def walkers(T, topo):
@@ -97,7 +103,7 @@ def fused(g, core, topo, dsts, srcs, outs, rsem, lsem):
 
 
 def window(T, f):
-    return T.win[:, 256 * f:256 * f + 256] if f > 1 else T.wins[:]
+    return T.win[:, 256 * f:256 * f + 256] if f < N - 1 else T.winu[:]
 
 
 def rank_program(g, core, T, topo):
@@ -118,6 +124,7 @@ def run_walker(g, core, q, k, T, topo, teams):
     w = K * q + k
     n_st = shares(T.cores[q], team, topo)[1]
     n_in = len(bits(topo.mask(team[0], core))) if k else shares(T.cores[1], [t[0] for t in teams], topo)[1]
+    labw, codw, labh, rhf, corr = (T.cols[:, i:i + 1] for i in range(5))
     nv = [0]
 
     def inc(ins):
@@ -129,27 +136,48 @@ def run_walker(g, core, q, k, T, topo, teams):
 
     v.memset(T.ones[:], 1.0).then_inc(sem["k1"], 1)
     v.memset(T.onesf[:], 1.0).then_inc(sem["k1"], 1)
-    v.memset(T.c16[:], 16.0).then_inc(sem["ce"], 1)
     g.iota(T.pi[:], [[0, 8]], 0, 1).then_inc(sem["k2"], 1)
     g.iota(T.ji[:], [[-1, 128]], 128, 1).then_inc(sem["k3"], 1)
+    g.iota(T.ni[:], [[1, 8]], 0, 0).then_inc(sem["k7"], 1)
     g.wait_ge(sem["k1"], 2)
-    g.affine_select(T.j1[:], T.onesf[:], [[-16, 8]], op.is_ge, 0.0, 0, 1).then_inc(sem["k4"], 1)
+    g.affine_select(T.ident[:], T.ones[:], [[-1, 128]], op.is_equal, 0.0, 0, 1).then_inc(sem["k6"], 1)
+    g.affine_select(T.j1[:], T.onesf[:, 0:8], [[-16, 8]], op.is_ge, 0.0, 0, 1).then_inc(sem["k4"], 1)
     g.wait_ge(sem["k4"], 1)
     g.affine_select(T.jm[:], T.j1[:], [[16, 8]], op.is_ge, 0.0, 15, -1).then_inc(sem["k5"], 1)
-    g.affine_select(T.ident[:], T.ones[:], [[-1, 128]], op.is_equal, 0.0, 0, 1).then_inc(sem["k6"], 1)
+    inc(v.memset(T.c16w[:], 16.0))
+    for buf, top, bot in ((T.c16h, 16.0, 0.0), (T.onest, 1.0, 0.0), (T.onesb, 0.0, 1.0), (T.w64, 64.0, 1.0)):
+        inc(v.memset(buf[0:64, :], top))
+        inc(v.memset(buf[64:128, :], bot))
+    inc(v.memset(T.fah[64:128, :], 0.0))
+    inc(v.memset(T.fbh[64:128, :], 0.0))
     v.wait_ge(sem["k2"], 1)
-    inc(v.tensor_scalar(T.hhp[:], T.pi[:], 7, None, op.bitwise_and))
-    inc(v.tensor_scalar(T.rp[:], T.pi[:], 3, None, op.logical_shift_right))
+    inc(v.tensor_scalar(T.hw[:], T.pi[:], 7, None, op.bitwise_and))
+    inc(v.tensor_scalar(T.rw[:], T.pi[:], 3, None, op.logical_shift_right))
+    inc(v.tensor_scalar(T.hh[:], T.pi[:], 3, None, op.bitwise_and))
+    inc(v.tensor_scalar(T.rh[:], T.pi[:], 2, 15, op.logical_shift_right, op.bitwise_and))
+    inc(v.tensor_scalar(T.pa[:], T.pi[:], 15, None, op.bitwise_and))
     v.wait_ge(sem["k3"], 1)
     inc(v.tensor_scalar(T.ja[:], T.ji[:], 15, None, op.bitwise_and))
+    v.wait_ge(sem["k7"], 1)
+    inc(v.tensor_copy(T.nof[:], T.ni[:]))
     flush()
-    v.tensor_scalar(T.fa[:], T.hhp[:], 2048.0, None, op.mult).then_inc(sem["ce"], 1)
-    inc(v.tensor_copy(T.fb[:], T.rp[:]))
-    v.tensor_scalar(T.e3b[:], T.ja[:], 0.0, None, op.is_equal).then_inc(sem["ce"], 1)
-    v.tensor_scalar(T.e3f[:], T.ja[:], 0.0, None, op.is_equal).then_inc(sem["ce"], 1)
+    inc(v.tensor_scalar(T.faw[:], T.hw[:], 2048.0, None, op.mult))
+    inc(v.tensor_copy(T.fbw[:], T.rw[:]))
+    inc(v.tensor_scalar(T.fah[0:64, :], T.hh[0:64, :], 4096.0, None, op.mult))
+    inc(v.tensor_copy(T.fbh[0:64, :], T.rh[0:64, :]))
+    inc(v.tensor_copy(rhf, T.rh[:, 0:1]))
+    inc(v.tensor_scalar(corr, T.pa[:, 0:1], 15.0, JUMP, op.not_equal, op.mult))
+    inc(v.tensor_scalar(T.da[:], T.ja[:], 0.0, DROP, op.is_equal, op.mult))
+    inc(v.tensor_scalar(T.db[:], T.ja[:], 15.0, JUMP, op.is_equal, op.mult))
+    inc(v.tensor_scalar(T.e3f[:], T.ja[:], 0.0, None, op.is_equal))
     flush()
-    inc(v.tensor_scalar(T.labp[:], T.hhp[:, 0:1], 16.0, T.fb[:, 0:1], op.mult, op.add))
+    inc(v.tensor_scalar(labw, T.hw[:, 0:1], 16.0, T.fbw[:, 0:1], op.mult, op.add))
+    inc(v.tensor_scalar(codw, T.hw[:, 0:1], 2048.0, T.fbw[:, 0:1], op.mult, op.add))
+    inc(v.tensor_scalar(labh, T.hh[:, 0:1], 16.0, rhf, op.mult, op.add))
+    inc(v.tensor_tensor(T.d0[:], T.da[:], T.db[:], op.add))
 
+    v.wait_ge(sem["k5"], 1)
+    v.wait_ge(sem["k6"], 1)
     v.wait_ge(sem["st0"], n_st)
     inc(v.tensor_scalar(T.za[:], T.zi[:], 15, None, op.bitwise_and))
     inc(v.tensor_scalar(T.zb[:], T.zi[:], 7, 112, op.logical_shift_right, op.bitwise_and))
@@ -157,88 +185,92 @@ def run_walker(g, core, q, k, T, topo, teams):
     flush()
     inc(v.tensor_tensor(T.zl[:], T.za[:], T.zb[:], op.add))
     v.tensor_copy(T.woffs[:], T.zc[:]).then_inc(sem["sof"], 1)
-    v.wait_ge(sem["k5"], 1)
     flush()
-    inc(v.tensor_tensor(T.zj[:], T.zl[:], T.jm[:], op.mult))
-    flush()
-    inc(v.tensor_reduce(T.labc[:], T.zj[:], AxisListType.X, op.add))
-    v.wait_ge(sem["k6"], 1)
-    flush()
-    v.tensor_scalar(T.gl[:], T.ident[:], T.labc[:], None, op.mult).then_inc(sem["sgl"], 1)
+    v.tensor_tensor(T.gl[:], T.zl[:, 0:8].indirect(T.nof[:, 0:8]), T.ident[:], op.mult).then_inc(sem["sgl"], 1)
 
     def next_mask(t):
+        lab = codw if t == 2 else labh if N - t in HALF else labw
         v.wait_ge(sem["sxl"], t)
-        v.tensor_scalar(T.mask[:], T.XL[:, 0:128], T.labp[:], None, op.is_equal).then_inc(sem["smk"], 1)
+        v.tensor_scalar(T.mask[:], T.XL[:, 0:128], lab, None, op.is_equal).then_inc(sem["smk"], 1)
 
     def state_spread(t):
-        if t > 0:
-            v.wait_ge(sem["scs"], t)
-            v.tensor_tensor(T.us[:], T.CS[:, 0:8], T.jm[:], op.mult).then_inc(sem["sus"], 1)
+        v.wait_ge(sem["scs"], t)
+        v.tensor_tensor(T.us[:], T.CS[:, 0:8], T.jm[:], op.mult).then_inc(sem["sus"], 1)
 
-    def offsets_out(t, bank, s, n):
-        if t > 0:
-            v.wait_ge(sem[s], n)
-            v.tensor_copy(T.zo[:, 8 * t - 8:8 * t], bank[:, 0:8]).then_inc(sem["szo"], 1)
+    def offsets_out(t):
+        v.wait_ge(sem["szs"], t)
+        v.tensor_copy(T.zo[:, 8 * t - 8:8 * t], T.ZS[:, 0:8]).then_inc(sem["szo"], 1)
 
     next_mask(1)
     for t in range(1, STEPS + 1):
         f = N - t
+        a = 256 * f
+        go = T["go%d" % (t % 2)]
+        o = T.woffs[:, 0:8]
         v.wait_ge(sem["map%d" % f], n_in)
+        if t == 1:
+            v.tensor_copy(T.m32[:], T.winu[:]).then_inc(sem["cv"], 1)
+            v.wait_ge(sem["cv"], 1)
+            v.tensor_scalar(T.c8[:], T.m32[:], 4, 127, op.logical_shift_right, op.bitwise_and).then_inc(sem["cv"], 1)
+            v.tensor_scalar(T.a8[:], T.m32[:], 14351, None, op.bitwise_and).then_inc(sem["ca"], 1)
+            v.wait_ge(sem["cv"], 2)
         v.wait_ge(sem["sof"], t)
         v.wait_ge(sem["smk"], t)
-        if f > 1:
-            a = 256 * f
-            go = T["go%d" % (t % 2)]
-            v.tensor_tensor(go[:], T.win[:, a:a + 128].indirect(T.woffs[:, 0:8]), T.mask[:],
-                            op.mult).then_inc(sem["sgo"], 1)
-            v.tensor_tensor(T.gl[:], T.win[:, a + 128:a + 256].indirect(T.woffs[:, 0:8]), T.mask[:],
-                            op.mult).then_inc(sem["sgl"], 1)
-            state_spread(t - 1)
-            v.wait_ge(sem["sc"], t)
-            v.tensor_tensor(T.ub[:], T.C[:, 0:8], T.jm[:], op.mult).then_inc(sem["su"], 1)
-            next_mask(t + 1)
-            v.wait_ge(sem["sz"], t)
-            v.tensor_copy(T.woffs[:], T.Z[:, 0:8]).then_inc(sem["sof"], 1)
+        if t == 1:
+            v.tensor_tensor(go[:], T.c8[:, 0:128].indirect(o), T.mask[:], op.mult).then_inc(sem["sgo"], 1)
+            v.wait_ge(sem["ca"], 1)
+            v.tensor_tensor(T.gs[:], T.a8[:, 0:128].indirect(o), T.mask[:], op.mult).then_inc(sem["sgl"], 1)
+        elif f in HALF:
+            v.tensor_tensor(go[:], T.win[:, a:a + 256].indirect(o), T.mask[:], op.mult).then_inc(sem["sgo"], 1)
         else:
-            v.tensor_tensor(T.gs[:], T.wins[:, 0:128].indirect(T.woffs[:, 0:8]), T.mask[:],
-                            op.mult).then_inc(sem["sgo"], 1)
+            v.tensor_tensor(go[:], T.win[:, a:a + 128].indirect(o), T.mask[:], op.mult).then_inc(sem["sgo"], 1)
+            v.tensor_tensor(T.gl[:], T.win[:, a + 128:a + 256].indirect(o), T.mask[:], op.mult).then_inc(sem["sgl"], 1)
+        if t > 2:
+            offsets_out(t - 2)
+        if t > 1:
             state_spread(t - 1)
-            v.wait_ge(sem["sc"], t)
-            v.tensor_tensor(T.u8[:], T.C[:, 0:8], T.jm[:], op.mult).then_inc(sem["sus"], 1)
-        offsets_out(t - 1, T.ZS, "szs", t - 1)
-    offsets_out(STEPS, T.Z, "sz", STEPS)
+        v.wait_ge(sem["sc"], t)
+        v.tensor_tensor_scan(T.xs[:], T.d0[:], T.CB[:, 0:128], 0.0, op.add, op.max).then_inc(sem["ssc"], 1)
+        if t < STEPS:
+            next_mask(t + 1)
+            v.wait_ge(sem["ssc"], t)
+            v.tensor_scalar(T.woffs[:], T.xs[:, 15:128:16], corr, None, op.subtract).then_inc(sem["sof"], 1)
+        else:
+            offsets_out(t - 1)
+            v.wait_ge(sem["ssc"], t)
+            v.tensor_scalar(T.zo[:, 8 * t - 8:8 * t], T.xs[:, 15:128:16], corr, None, op.subtract).then_inc(sem["szo"], 1)
 
     pe.wait_ge(sem["k1"], 2)
-    pe.wait_ge(sem["ce"], 4)
     pe.wait_ge(sem["v"], nv[0])
     pe.wait_ge(sem["sgl"], 1)
     pe.matmul(T.XL[:, 0:128], T.ones[:], T.gl[:], True, True).then_inc(sem["sxl"], 1)
-    for t in range(1, STEPS):
+    n_gl = 1
+    for t in range(1, STEPS + 1):
+        f = N - t
         go = T["go%d" % (t % 2)]
+        lhs = T.w64 if f == 1 else T.onest if f in HALF else T.ones
         pe.wait_ge(sem["sgo"], t)
-        pe.matmul(T.C[:, 0:8], go[:], T.ones[:, 0:8], True, True).then_inc(sem["sc"], 1)
-        pe.wait_ge(sem["sgl"], t + 1)
-        pe.matmul(T.XL[:, 0:128], T.ones[:], T.gl[:], True, True).then_inc(sem["sxl"], 1)
-        pe.wait_ge(sem["su"], t)
-        pe.matmul(T.Z[:, 0:8], T.e3b[:], T.ub[:], True, True).then_inc(sem["sz"], 1)
+        pe.matmul(T.CB[:, 0:128], lhs[:], go[:], True, True).then_inc(sem["sc"], 1)
+        if 1 < f and f in HALF:
+            pe.matmul(T.XL[:, 0:128], T.onesb[:], go[:], True, True).then_inc(sem["sxl"], 1)
+        elif f > 1:
+            n_gl += 1
+            pe.wait_ge(sem["sgl"], n_gl)
+            lt, rt = (T.onesf, T.gs) if t == 1 else (T.ones, T.gl)
+            pe.matmul(T.XL[:, 0:128], lt[:], rt[:], True, True).then_inc(sem["sxl"], 1)
         if t > 1:
             pe.wait_ge(sem["sus"], t - 1)
             if t > 2:
                 pe.wait_ge(sem["szo"], t - 2)
             pe.matmul(T.ZS[:, 0:8], T.e3f[:], T.us[:], True, True).then_inc(sem["szs"], 1)
-        pe.wait_ge(sem["smk"], t + 1)
-        pe.matmul(T.CS[:, 0:8], go[:], T.c16[:], True, False)
-        pe.matmul(T.CS[:, 0:8], T.mask[:], T.fa[:], False, False)
-        pe.matmul(T.CS[:, 0:8], T.mask[:], T.fb[:], False, True).then_inc(sem["scs"], 1)
-    pe.wait_ge(sem["sgo"], STEPS)
-    pe.matmul(T.C[:, 0:8], T.gs[:], T.onesf[:], True, True).then_inc(sem["sc"], 1)
-    pe.wait_ge(sem["sus"], STEPS - 1)
-    pe.wait_ge(sem["szo"], STEPS - 2)
-    pe.matmul(T.ZS[:, 0:8], T.e3f[:], T.us[:], True, True).then_inc(sem["szs"], 1)
-    pe.wait_ge(sem["sus"], STEPS)
-    pe.matmul(T.Z[:, 0:8], T.e3f[:], T.u8[:], True, True).then_inc(sem["sz"], 1)
+        if f > 1:
+            fa, fb = (T.fah, T.fbh) if f - 1 in HALF else (T.faw, T.fbw)
+            pe.wait_ge(sem["smk"], t + 1)
+            pe.matmul(T.CS[:, 0:8], go[:], T.c16h[:] if f in HALF else T.c16w[:], True, False)
+            pe.matmul(T.CS[:, 0:8], T.mask[:], fa[:], False, False)
+            pe.matmul(T.CS[:, 0:8], T.mask[:], fb[:], False, True).then_inc(sem["scs"], 1)
 
-    sent, passed = 0, 0
+    sent, passed = [0], [0]
 
     def forward(f):
         g.wait_ge(sem["map%d" % f], n_in)
@@ -246,24 +278,24 @@ def run_walker(g, core, q, k, T, topo, teams):
         g.remote_dma_fused([RemoteDMATransfer(dst_ids=[dst_id(topo, d) for d in team[1:]], dma_engine_mask=m,
                                               remote_sem=sem["map%d" % f], srcs=[window(T, f)],
                                               dsts=[window(T, f)] * (K - 1), alu_op=0)], local_sem=sem["fwd"])
-        return len(bits(m))
+        passed[0] += len(bits(m))
 
     if k == 0:
         for f in range(N - 1, N - 1 - AHEAD, -1):
-            passed += forward(f)
+            forward(f)
     for t in range(1, STEPS + 1):
         g.wait_ge(sem["szo"], t)
         dst = T.cores[N - 1 - t]
         m = topo.mask(core, dst)
         rid, pid, _ = topo.addr(dst)
         g.remote_dma(T.offs[:, 8 * w:8 * w + 8], T.zo[:, 8 * t - 8:8 * t], sem["lin"], sem["snt"], pid, rid, m)
-        sent += len(bits(m))
+        sent[0] += len(bits(m))
         f = N - AHEAD - t
         if k == 0 and f >= 1:
-            passed += forward(f)
-    g.wait_ge(sem["snt"], sent)
-    if passed:
-        g.wait_ge(sem["fwd"], passed)
+            forward(f)
+    g.wait_ge(sem["snt"], sent[0])
+    if passed[0]:
+        g.wait_ge(sem["fwd"], passed[0])
 
 
 def run_rank(g, core, rank, T, topo, teams):
@@ -271,70 +303,110 @@ def run_rank(g, core, rank, T, topo, teams):
     v, a, sy = g.vector, g.scalar, g.sync
     op = AluOpType
     lister = rank < Q
+    half = rank in HALF
 
     F = FIRST[rank]
-    if lister or rank == N - 1:
+    if lister:
+        x = 8 * K * rank
         for i in range(8):
-            e = sy if lister and i % 2 else a
-            e.dma_start(T.st8[16 * i:16 * i + 16, :], T.st[:]).then_inc(sem["lds"], 16)
-    if rank > 0:
-        sy.dma_start(T.vb[:], T.bp[:]).then_inc(sem["ldb"], 16)
+            e = sy if i % 2 else a
+            e.dma_start(T.st8[16 * i:16 * i + 16, x:x + 8 * K], T.st[:, x:x + 8 * K]).then_inc(sem["lds"], 16)
+    n_b = 0
+    if half:
+        for p in (0, 64):
+            sy.dma_start(T.vb[p:p + 64, :], T.bp[:]).then_inc(sem["ldb"], 16)
+        n_b = 32
+    elif rank > 0:
+        sy.dma_start(T.vb[:, 0:128], T.bp[:]).then_inc(sem["ldb"], 16)
+        n_b = 16
     if lister:
         g.wait_ge(sem["lds"], 128)
-        n = fused(g, core, topo, teams[rank],
-                  [T.st8[:, 8 * w:8 * w + 8] for w in range(K * rank, K * rank + K)], [T.zi[:]] * K,
+        n = fused(g, core, topo, teams[rank], [T.st8[:, x + 8 * k:x + 8 * k + 8] for k in range(K)], [T.zi[:]] * K,
                   sem["st0"], sem["snl"])
         sy.wait_ge(sem["snl"], n)
     sy.dma_start(T.tabw[:, 0:F], T.tab[:, 0:F]).then_inc(sem["lda"], 16)
+    n_t = 16
+    if 0 < rank < HOLD:
+        sy.dma_start(T.tabw[:, F:F + SECOND], T.tab[:, F:F + SECOND]).then_inc(sem["ldt"], 16)
+        F += SECOND
+        n_t = 32
 
     if rank > 0:
-        if rank > 1:
-            v.wait_ge(sem["ldb"], 16)
-            v.tensor_scalar(T.t1[:], T.vb[:], 15, None, op.bitwise_and).then_inc(sem["v"], 1)
-            v.tensor_scalar(T.t2[:], T.vb[:], 7, 112, op.logical_shift_right, op.bitwise_and).then_inc(sem["v"], 1)
-            v.tensor_scalar(T.u0[:], T.vb[:], 4, 127, op.logical_shift_right, op.bitwise_and).then_inc(sem["v"], 1)
-            v.wait_ge(sem["v"], 2)
-            v.tensor_tensor(T.wout[:, 128:256], T.t1[:], T.t2[:], op.add).then_inc(sem["enc"], 1)
-            v.wait_ge(sem["v"], 3)
-            v.tensor_copy(T.wout[:, 0:128], T.u0[:]).then_inc(sem["enc"], 1)
-            g.wait_ge(sem["enc"], 2)
+        if half:
+            s_c, m_l = (4, 15) if rank > 1 else (6, 63)
+            t_, b_ = slice(0, 64), slice(64, 128)
+            src = T.wout[:]
+            if rank > 1:
+                v.memset(T.ty[t_, :], 0).then_inc(sem["v"], 1)
+            v.wait_ge(sem["ldb"], n_b)
+            v.tensor_scalar(T.tx[t_, :], T.vb[t_, :], s_c, 255, op.logical_shift_right, op.bitwise_and).then_inc(sem["v"], 1)
+            v.tensor_scalar(T.tx[b_, :], T.vb[b_, :], m_l, None, op.bitwise_and).then_inc(sem["v"], 1)
+            if rank > 1:
+                v.tensor_scalar(T.ty[b_, :], T.vb[b_, :], 8, 48, op.logical_shift_right,
+                                op.bitwise_and).then_inc(sem["v"], 1)
+                v.wait_ge(sem["v"], 4)
+                v.tensor_tensor(T.wout[:], T.tx[:], T.ty[:], op.add).then_inc(sem["enc"], 1)
+            else:
+                v.wait_ge(sem["v"], 2)
+                v.tensor_copy(T.wout[:], T.tx[:]).then_inc(sem["enc"], 1)
+            g.wait_ge(sem["enc"], 1)
+        elif rank == N - 1:
+            src = T.wu[:]
+            v.wait_ge(sem["ldb"], n_b)
+            v.tensor_copy(T.wu[:], T.vb[:, 0:128]).then_inc(sem["enc"], 1)
+            g.wait_ge(sem["enc"], 1)
         else:
-            g.wait_ge(sem["ldb"], 16)
+            src = T.wout[:]
+            x, y = T.tx[:, 0:128], T.ty[:, 0:128]
+            v.wait_ge(sem["ldb"], n_b)
+            v.tensor_scalar(x, T.vb[:, 0:128], 15, None, op.bitwise_and).then_inc(sem["v"], 1)
+            v.tensor_scalar(y, T.vb[:, 0:128], 8, 48, op.logical_shift_right, op.bitwise_and).then_inc(sem["v"], 1)
+            v.tensor_scalar(T.tz[:], T.vb[:, 0:128], 4, 255, op.logical_shift_right, op.bitwise_and).then_inc(sem["v"], 1)
+            v.wait_ge(sem["v"], 3)
+            v.tensor_tensor(T.wout[:, 128:256], x, y, op.add).then_inc(sem["enc"], 1)
+            v.tensor_copy(T.wout[:, 0:128], T.tz[:]).then_inc(sem["enc"], 1)
+            g.wait_ge(sem["enc"], 2)
         if rank < HOLD:
             g.wait_ge(sem["lda"], 16)
-        n = fused(g, core, topo, [t[0] for t in teams], [T.wout[:] if rank > 1 else T.vb[:]] * Q,
-                  [window(T, rank)] * Q, sem["map%d" % rank], sem["snt"])
+        n = fused(g, core, topo, [t[0] for t in teams], [src] * Q, [window(T, rank)] * Q, sem["map%d" % rank], sem["snt"])
         sy.wait_ge(sem["snt"], n)
 
     sy.dma_start(T.tabw[:, F:], T.tab[:, F:]).then_inc(sem["ldt"], 16)
 
     if rank == N - 1:
+        a.wait_ge(sem["snt"], n)
+        for i in range(8):
+            a.dma_start(T.st8[16 * i:16 * i + 16, :], T.st[:]).then_inc(sem["lds"], 16)
         v.wait_ge(sem["lds"], 128)
         v.tensor_copy(T.offs[:], T.st8[:]).then_inc(sem["ofr"], 1)
         got, n_in = sem["ofr"], 1
     else:
         got, n_in = sem["lin"], sum(len(bits(topo.mask(w, core))) for team in teams for w in team)
 
-    H = 1024
-    cut = [(0, 384), (384, H), (H, H + 384), (H + 384, 2 * H)]
+    n_p = len(PIECES)
+    cut, x = [], 0
+    for c in PIECES + PIECES:
+        cut.append((x, x + c))
+        x += c
 
-    def part(k):
-        x, y = cut[k]
+    def part(i):
+        x, y = cut[i]
         return T.yb[:, x:y], T.tabw[:, 0:16384].indirect(T.offs[:, x // 16:y // 16])
 
     for e in (v, a):
         e.wait_ge(sem["lda"], 16)
-        e.wait_ge(sem["ldt"], 16)
+        e.wait_ge(sem["ldt"], n_t)
         e.wait_ge(got, n_in)
-    for k in (0, 1):
-        o, i = part(k)
-        v.tensor_copy(o, i).then_inc(sem["yd%d" % k], 1)
-    for k in (2, 3):
-        o, i = part(k)
-        a.activation(o, i, ActivationFunctionType.Copy).then_inc(sem["yd%d" % k], 1)
-    for k in (0, 2, 1, 3):
-        e = a if k == 3 else sy
-        x, y = cut[k]
-        e.wait_ge(sem["yd%d" % k], 1)
-        e.dma_start(T.y[:, x:y], T.yb[:, x:y]).then_inc(sem["sto"], 16)
-    sy.wait_ge(sem["sto"], 64)
+    for i in range(n_p):
+        o, s = part(i)
+        v.tensor_copy(o, s).then_inc(sem["yd%d" % i], 1)
+    for i in range(n_p, 2 * n_p):
+        o, s = part(i)
+        a.activation(o, s, ActivationFunctionType.Copy).then_inc(sem["yd%d" % i], 1)
+    for i in range(n_p):
+        for j in (i, n_p + i):
+            e = a if j == 2 * n_p - 1 else sy
+            x, y = cut[j]
+            e.wait_ge(sem["yd%d" % j], 1)
+            e.dma_start(T.y[:, x:y], T.yb[:, x:y]).then_inc(sem["sto"], 16)
+    sy.wait_ge(sem["sto"], 32 * n_p)

@@ -7,13 +7,14 @@ Q = 4
 K = 4
 STEPS = N - 1
 HALF = range(1, N - 2)
-FIRST = [2048, 4096, 3584, 3072, 2816, 2048, 1536, 1024, 512]
-SECOND = 1024
+FIRST = [2048, 4096, 3584, 3072, 2816, 2048, 1536, 1536, 1024]
+SECOND = 1536
 HOLD = N - 2
 AHEAD = 7
 JUMP = 16384.0
 DROP = -1048576.0
 PIECES = [320, 384, 320]
+CHAINS = (0, 1)
 
 SCRATCH = {
     "tabw": ("sbuf", [128, 16384], "bfloat16"),
@@ -33,7 +34,7 @@ SCRATCH = {
     "zo": ("sbuf", [128, 8 * STEPS], "uint16"),
     "cols": ("sbuf", [128, 5], "float32"),
 }
-for _k in ("ji", "ja", "m32", "c8", "a8"):
+for _k in ("ji", "m32", "c8", "a8"):
     SCRATCH[_k] = ("sbuf", [128, 128], "int32")
 for _k in ("e3f", "gs", "onesf", "da", "db", "d0", "xs"):
     SCRATCH[_k] = ("sbuf", [128, 128], "float32")
@@ -45,12 +46,12 @@ for _k in ("c16w", "faw", "fbw", "c16h", "fah", "fbh"):
     SCRATCH[_k] = ("sbuf", [128, 8], "bfloat16")
 for _k in ("ones", "onest", "onesb", "w64", "ident", "go0", "go1", "gl", "mask"):
     SCRATCH[_k] = ("sbuf", [128, 128], "bfloat16")
-for _k in ("CB", "XL", "CS", "ZS"):
+for _k in ("CB0", "CB1", "XL0", "XL1", "CS", "ZS"):
     SCRATCH[_k] = ("psum", [128, 512], "float32")
 
 SEMAPHORES = (["ldb", "lda", "ldt", "lds", "v", "enc", "snt", "snl", "fwd", "lin", "ofr", "sto", "st0", "k1", "k2", "k3",
-               "k4", "k5", "k6", "k7", "cv", "ca",
-               "sgo", "sgl", "sc", "sxl", "ssc", "smk", "sof", "scs", "sus", "szs", "szo"]
+               "k4", "k5", "k6", "k7", "cv", "ca", "sgl", "scs", "sus", "szs", "szo"]
+              + ["%s%d" % (s, c) for s in ("sgo", "sgl", "sc", "sxl", "ssc", "smk", "sof") for c in CHAINS]
               + ["yd%d" % i for i in range(2 * len(PIECES))] + ["map%d" % f for f in range(1, N)])
 
 
@@ -125,7 +126,12 @@ def run_walker(g, core, q, k, T, topo, teams):
     n_st = shares(T.cores[q], team, topo)[1]
     n_in = len(bits(topo.mask(team[0], core))) if k else shares(T.cores[1], [t[0] for t in teams], topo)[1]
     labw, codw, labh, rhf, corr = (T.cols[:, i:i + 1] for i in range(5))
+    J = (slice(0, 64), slice(64, 128))
+    O = (slice(0, 4), slice(4, 8))
     nv = [0]
+
+    def S(name, c):
+        return sem["%s%d" % (name, c)]
 
     def inc(ins):
         ins.then_inc(sem["v"], 1)
@@ -157,7 +163,7 @@ def run_walker(g, core, q, k, T, topo, teams):
     inc(v.tensor_scalar(T.rh[:], T.pi[:], 2, 15, op.logical_shift_right, op.bitwise_and))
     inc(v.tensor_scalar(T.pa[:], T.pi[:], 15, None, op.bitwise_and))
     v.wait_ge(sem["k3"], 1)
-    inc(v.tensor_scalar(T.ja[:], T.ji[:], 15, None, op.bitwise_and))
+    inc(v.tensor_scalar(T.ji[:], T.ji[:], 15, None, op.bitwise_and))
     v.wait_ge(sem["k7"], 1)
     inc(v.tensor_copy(T.nof[:], T.ni[:]))
     flush()
@@ -167,9 +173,9 @@ def run_walker(g, core, q, k, T, topo, teams):
     inc(v.tensor_copy(T.fbh[0:64, :], T.rh[0:64, :]))
     inc(v.tensor_copy(rhf, T.rh[:, 0:1]))
     inc(v.tensor_scalar(corr, T.pa[:, 0:1], 15.0, JUMP, op.not_equal, op.mult))
-    inc(v.tensor_scalar(T.da[:], T.ja[:], 0.0, DROP, op.is_equal, op.mult))
-    inc(v.tensor_scalar(T.db[:], T.ja[:], 15.0, JUMP, op.is_equal, op.mult))
-    inc(v.tensor_scalar(T.e3f[:], T.ja[:], 0.0, None, op.is_equal))
+    inc(v.tensor_scalar(T.da[:], T.ji[:], 0.0, DROP, op.is_equal, op.mult))
+    inc(v.tensor_scalar(T.db[:], T.ji[:], 15.0, JUMP, op.is_equal, op.mult))
+    inc(v.tensor_scalar(T.e3f[:], T.ji[:], 0.0, None, op.is_equal))
     flush()
     inc(v.tensor_scalar(labw, T.hw[:, 0:1], 16.0, T.fbw[:, 0:1], op.mult, op.add))
     inc(v.tensor_scalar(codw, T.hw[:, 0:1], 2048.0, T.fbw[:, 0:1], op.mult, op.add))
@@ -184,14 +190,15 @@ def run_walker(g, core, q, k, T, topo, teams):
     inc(v.tensor_scalar(T.zc[:], T.zi[:], 4, 127, op.logical_shift_right, op.bitwise_and))
     flush()
     inc(v.tensor_tensor(T.zl[:], T.za[:], T.zb[:], op.add))
-    v.tensor_copy(T.woffs[:], T.zc[:]).then_inc(sem["sof"], 1)
+    for c in CHAINS:
+        v.tensor_copy(T.woffs[:, O[c]], T.zc[:, O[c]]).then_inc(S("sof", c), 1)
     flush()
     v.tensor_tensor(T.gl[:], T.zl[:, 0:8].indirect(T.nof[:, 0:8]), T.ident[:], op.mult).then_inc(sem["sgl"], 1)
 
-    def next_mask(t):
+    def next_mask(t, c):
         lab = codw if t == 2 else labh if N - t in HALF else labw
-        v.wait_ge(sem["sxl"], t)
-        v.tensor_scalar(T.mask[:], T.XL[:, 0:128], lab, None, op.is_equal).then_inc(sem["smk"], 1)
+        v.wait_ge(S("sxl", c), t)
+        v.tensor_scalar(T.mask[:, J[c]], T["XL%d" % c][:, 0:64], lab, None, op.is_equal).then_inc(S("smk", c), 1)
 
     def state_spread(t):
         v.wait_ge(sem["scs"], t)
@@ -201,12 +208,12 @@ def run_walker(g, core, q, k, T, topo, teams):
         v.wait_ge(sem["szs"], t)
         v.tensor_copy(T.zo[:, 8 * t - 8:8 * t], T.ZS[:, 0:8]).then_inc(sem["szo"], 1)
 
-    next_mask(1)
+    for c in CHAINS:
+        next_mask(1, c)
     for t in range(1, STEPS + 1):
         f = N - t
         a = 256 * f
         go = T["go%d" % (t % 2)]
-        o = T.woffs[:, 0:8]
         v.wait_ge(sem["map%d" % f], n_in)
         if t == 1:
             v.tensor_copy(T.m32[:], T.winu[:]).then_inc(sem["cv"], 1)
@@ -214,50 +221,63 @@ def run_walker(g, core, q, k, T, topo, teams):
             v.tensor_scalar(T.c8[:], T.m32[:], 4, 127, op.logical_shift_right, op.bitwise_and).then_inc(sem["cv"], 1)
             v.tensor_scalar(T.a8[:], T.m32[:], 14351, None, op.bitwise_and).then_inc(sem["ca"], 1)
             v.wait_ge(sem["cv"], 2)
-        v.wait_ge(sem["sof"], t)
-        v.wait_ge(sem["smk"], t)
-        if t == 1:
-            v.tensor_tensor(go[:], T.c8[:, 0:128].indirect(o), T.mask[:], op.mult).then_inc(sem["sgo"], 1)
-            v.wait_ge(sem["ca"], 1)
-            v.tensor_tensor(T.gs[:], T.a8[:, 0:128].indirect(o), T.mask[:], op.mult).then_inc(sem["sgl"], 1)
-        elif f in HALF:
-            v.tensor_tensor(go[:], T.win[:, a:a + 256].indirect(o), T.mask[:], op.mult).then_inc(sem["sgo"], 1)
-        else:
-            v.tensor_tensor(go[:], T.win[:, a:a + 128].indirect(o), T.mask[:], op.mult).then_inc(sem["sgo"], 1)
-            v.tensor_tensor(T.gl[:], T.win[:, a + 128:a + 256].indirect(o), T.mask[:], op.mult).then_inc(sem["sgl"], 1)
+        for c in CHAINS:
+            o = T.woffs[:, O[c]]
+            mk = T.mask[:, J[c]]
+            v.wait_ge(S("sof", c), t)
+            v.wait_ge(S("smk", c), t)
+            if t == 1:
+                v.tensor_tensor(go[:, J[c]], T.c8[:, 0:128].indirect(o), mk, op.mult).then_inc(S("sgo", c), 1)
+                v.wait_ge(sem["ca"], 1)
+                v.tensor_tensor(T.gs[:, J[c]], T.a8[:, 0:128].indirect(o), mk, op.mult).then_inc(S("sgl", c), 1)
+            elif f in HALF:
+                v.tensor_tensor(go[:, J[c]], T.win[:, a:a + 256].indirect(o), mk, op.mult).then_inc(S("sgo", c), 1)
+            else:
+                v.tensor_tensor(go[:, J[c]], T.win[:, a:a + 128].indirect(o), mk, op.mult).then_inc(S("sgo", c), 1)
+                v.tensor_tensor(T.gl[:, J[c]], T.win[:, a + 128:a + 256].indirect(o), mk,
+                                op.mult).then_inc(S("sgl", c), 1)
         if t > 2:
             offsets_out(t - 2)
         if t > 1:
             state_spread(t - 1)
-        v.wait_ge(sem["sc"], t)
-        v.tensor_tensor_scan(T.xs[:], T.d0[:], T.CB[:, 0:128], 0.0, op.add, op.max).then_inc(sem["ssc"], 1)
-        if t < STEPS:
-            next_mask(t + 1)
-            v.wait_ge(sem["ssc"], t)
-            v.tensor_scalar(T.woffs[:], T.xs[:, 15:128:16], corr, None, op.subtract).then_inc(sem["sof"], 1)
-        else:
+        for c in CHAINS:
+            v.wait_ge(S("sc", c), t)
+            v.tensor_tensor_scan(T.xs[:, J[c]], T.d0[:, J[c]], T["CB%d" % c][:, 0:64], 0.0, op.add,
+                                 op.max).then_inc(S("ssc", c), 1)
+        if t == STEPS:
             offsets_out(t - 1)
-            v.wait_ge(sem["ssc"], t)
-            v.tensor_scalar(T.zo[:, 8 * t - 8:8 * t], T.xs[:, 15:128:16], corr, None, op.subtract).then_inc(sem["szo"], 1)
+        for c in CHAINS:
+            x = 64 * c
+            if t < STEPS:
+                next_mask(t + 1, c)
+            v.wait_ge(S("ssc", c), t)
+            if t < STEPS:
+                v.tensor_scalar(T.woffs[:, O[c]], T.xs[:, x + 15:x + 64:16], corr, None,
+                                op.subtract).then_inc(S("sof", c), 1)
+            else:
+                z = 8 * t - 8 + 4 * c
+                v.tensor_scalar(T.zo[:, z:z + 4], T.xs[:, x + 15:x + 64:16], corr, None,
+                                op.subtract).then_inc(sem["szo"], 1)
 
     pe.wait_ge(sem["k1"], 2)
     pe.wait_ge(sem["v"], nv[0])
     pe.wait_ge(sem["sgl"], 1)
-    pe.matmul(T.XL[:, 0:128], T.ones[:], T.gl[:], True, True).then_inc(sem["sxl"], 1)
-    n_gl = 1
+    for c in CHAINS:
+        pe.matmul(T["XL%d" % c][:, 0:64], T.ones[:], T.gl[:, J[c]], True, True).then_inc(S("sxl", c), 1)
     for t in range(1, STEPS + 1):
         f = N - t
         go = T["go%d" % (t % 2)]
         lhs = T.w64 if f == 1 else T.onest if f in HALF else T.ones
-        pe.wait_ge(sem["sgo"], t)
-        pe.matmul(T.CB[:, 0:128], lhs[:], go[:], True, True).then_inc(sem["sc"], 1)
-        if 1 < f and f in HALF:
-            pe.matmul(T.XL[:, 0:128], T.onesb[:], go[:], True, True).then_inc(sem["sxl"], 1)
-        elif f > 1:
-            n_gl += 1
-            pe.wait_ge(sem["sgl"], n_gl)
-            lt, rt = (T.onesf, T.gs) if t == 1 else (T.ones, T.gl)
-            pe.matmul(T.XL[:, 0:128], lt[:], rt[:], True, True).then_inc(sem["sxl"], 1)
+        for c in CHAINS:
+            xl = T["XL%d" % c][:, 0:64]
+            pe.wait_ge(S("sgo", c), t)
+            pe.matmul(T["CB%d" % c][:, 0:64], lhs[:], go[:, J[c]], True, True).then_inc(S("sc", c), 1)
+            if 1 < f and f in HALF:
+                pe.matmul(xl, T.onesb[:], go[:, J[c]], True, True).then_inc(S("sxl", c), 1)
+            elif f > 1:
+                pe.wait_ge(S("sgl", c), t)
+                lt, rt = (T.onesf, T.gs) if t == 1 else (T.ones, T.gl)
+                pe.matmul(xl, lt[:], rt[:, J[c]], True, True).then_inc(S("sxl", c), 1)
         if t > 1:
             pe.wait_ge(sem["sus"], t - 1)
             if t > 2:
@@ -265,7 +285,8 @@ def run_walker(g, core, q, k, T, topo, teams):
             pe.matmul(T.ZS[:, 0:8], T.e3f[:], T.us[:], True, True).then_inc(sem["szs"], 1)
         if f > 1:
             fa, fb = (T.fah, T.fbh) if f - 1 in HALF else (T.faw, T.fbw)
-            pe.wait_ge(sem["smk"], t + 1)
+            for c in CHAINS:
+                pe.wait_ge(S("smk", c), t + 1)
             pe.matmul(T.CS[:, 0:8], go[:], T.c16h[:] if f in HALF else T.c16w[:], True, False)
             pe.matmul(T.CS[:, 0:8], T.mask[:], fa[:], False, False)
             pe.matmul(T.CS[:, 0:8], T.mask[:], fb[:], False, True).then_inc(sem["scs"], 1)
@@ -284,7 +305,7 @@ def run_walker(g, core, q, k, T, topo, teams):
         for f in range(N - 1, N - 1 - AHEAD, -1):
             forward(f)
     for t in range(1, STEPS + 1):
-        g.wait_ge(sem["szo"], t)
+        g.wait_ge(sem["szo"], t if t < STEPS else STEPS - 1 + len(CHAINS))
         dst = T.cores[N - 1 - t]
         m = topo.mask(core, dst)
         rid, pid, _ = topo.addr(dst)

from concourse.bass import DstId, RemoteDMATransfer
from concourse.mybir import AluOpType, ActivationFunctionType

N = 9
NCORES = 112
Q = 4
K = 4
STEPS = N - 1
HALF = range(1, N - 2)
FIRST = [2048, 4096, 3584, 3072, 2816, 2048, 1536, 1536, 1024]
SECOND = 1536
HOLD = N - 2
AHEAD = 7
JUMP = 16384.0
DROP = -1048576.0
PIECES = [320, 384, 320]
CHAINS = (0, 1)

SCRATCH = {
    "tabw": ("sbuf", [128, 16384], "bfloat16"),
    "yb": ("sbuf", [128, 2048], "bfloat16"),
    "vb": ("sbuf", [128, 256], "int32"),
    "tx": ("sbuf", [128, 256], "int32"),
    "ty": ("sbuf", [128, 256], "int32"),
    "tz": ("sbuf", [128, 128], "int32"),
    "wout": ("sbuf", [128, 256], "bfloat16"),
    "wu": ("sbuf", [128, 128], "uint16"),
    "st8": ("sbuf", [128, 128], "int32"),
    "offs": ("sbuf", [128, 128], "uint16"),
    "win": ("sbuf", [128, 256 * (N - 1)], "bfloat16"),
    "winu": ("sbuf", [128, 128], "uint16"),
    "woffs": ("sbuf", [128, 8], "uint16"),
    "nof": ("sbuf", [128, 8], "uint16"),
    "zo": ("sbuf", [128, 8 * STEPS], "uint16"),
    "cols": ("sbuf", [128, 5], "float32"),
}
for _k in ("ji", "m32", "c8", "a8"):
    SCRATCH[_k] = ("sbuf", [128, 128], "int32")
for _k in ("e3f", "gs", "onesf", "da", "db", "d0", "xs"):
    SCRATCH[_k] = ("sbuf", [128, 128], "float32")
for _k in ("pi", "ni", "hw", "rw", "hh", "rh", "pa", "zi", "za", "zb", "zc"):
    SCRATCH[_k] = ("sbuf", [128, 8], "int32")
for _k in ("j1", "jm", "zl", "us"):
    SCRATCH[_k] = ("sbuf", [128, 8], "float32")
for _k in ("c16w", "faw", "fbw", "c16h", "fah", "fbh"):
    SCRATCH[_k] = ("sbuf", [128, 8], "bfloat16")
for _k in ("ones", "onest", "onesb", "w64", "ident", "go0", "go1", "gl", "mask"):
    SCRATCH[_k] = ("sbuf", [128, 128], "bfloat16")
for _k in ("CB0", "CB1", "XL0", "XL1", "CS", "ZS"):
    SCRATCH[_k] = ("psum", [128, 512], "float32")

SEMAPHORES = (["ldb", "lda", "ldt", "lds", "v", "enc", "snt", "snl", "fwd", "lin", "ofr", "sto", "st0", "k1", "k2", "k3",
               "k4", "k5", "k6", "k7", "cv", "ca", "sgl", "scs", "sus", "szs", "szo"]
              + ["%s%d" % (s, c) for s in ("sgo", "sgl", "sc", "sxl", "ssc", "smk", "sof") for c in CHAINS]
              + ["yd%d" % i for i in range(2 * len(PIECES))] + ["map%d" % f for f in range(1, N)])


def walkers(T, topo):
    ranks = list(T.cores)
    used = [topo.chip(c) for c in ranks]
    ok = {}
    for c in range(NCORES):
        if topo.chip(c) not in used and all(topo.may_write(c, r) for r in ranks):
            ok.setdefault(topo.chip(c), []).append(c)
    planes, out, i = [], [], 0
    for ch in sorted(ok):
        ok[ch].sort(key=lambda c: (topo.die(c) != topo.die(ranks[0]), c))
        for pl in planes:
            if topo.same_plane(pl[0], ch):
                pl.append(ch)
                break
        else:
            planes.append([ch])
    while len(out) < Q:
        out += [pl[i] for pl in planes if i < len(pl)]
        i += 1
    return [ok[ch][:K] for ch in out[:Q]]


def bits(m):
    return [1 << i for i in range(16) if m >> i & 1]


def shares(src, dsts, topo):
    m = topo.mask(src, dsts[0])
    for d in dsts:
        m &= topo.mask(src, d)
    e = bits(m)
    n = len(e) // len(dsts)
    return [sum(e[i * n:(i + 1) * n]) for i in range(len(dsts))], n


def dst_id(topo, d):
    rid, pid, _ = topo.addr(d)
    return DstId(rid=rid, pnc=pid)


def fused(g, core, topo, dsts, srcs, outs, rsem, lsem):
    masks, n = shares(core, dsts, topo)
    tr = [RemoteDMATransfer(dst_ids=[dst_id(topo, d)], dma_engine_mask=m, remote_sem=rsem, srcs=[s], dsts=[o], alu_op=0)
          for d, m, s, o in zip(dsts, masks, srcs, outs)]
    g.remote_dma_fused(tr, local_sem=lsem)
    return n * len(dsts)


def window(T, f):
    return T.win[:, 256 * f:256 * f + 256] if f < N - 1 else T.winu[:]


def rank_program(g, core, T, topo):
    teams = walkers(T, topo)
    rank = T.rank_of(core)
    if rank is not None:
        run_rank(g, core, rank, T, topo, teams)
    for q, team in enumerate(teams):
        if core in team:
            run_walker(g, core, q, team.index(core), T, topo, teams)


def run_walker(g, core, q, k, T, topo, teams):
    sem = T.sem
    v, pe = g.vector, g.tensor
    op = AluOpType
    team = teams[q]
    w = K * q + k
    n_st = shares(T.cores[q], team, topo)[1]
    n_in = len(bits(topo.mask(team[0], core))) if k else shares(T.cores[1], [t[0] for t in teams], topo)[1]
    labw, codw, labh, rhf, corr = (T.cols[:, i:i + 1] for i in range(5))
    J = (slice(0, 64), slice(64, 128))
    O = (slice(0, 4), slice(4, 8))
    nv = [0]

    def S(name, c):
        return sem["%s%d" % (name, c)]

    def inc(ins):
        ins.then_inc(sem["v"], 1)
        nv[0] += 1

    def flush():
        v.wait_ge(sem["v"], nv[0])

    v.memset(T.ones[:], 1.0).then_inc(sem["k1"], 1)
    v.memset(T.onesf[:], 1.0).then_inc(sem["k1"], 1)
    g.iota(T.pi[:], [[0, 8]], 0, 1).then_inc(sem["k2"], 1)
    g.iota(T.ji[:], [[-1, 128]], 128, 1).then_inc(sem["k3"], 1)
    g.iota(T.ni[:], [[1, 8]], 0, 0).then_inc(sem["k7"], 1)
    g.wait_ge(sem["k1"], 2)
    g.affine_select(T.ident[:], T.ones[:], [[-1, 128]], op.is_equal, 0.0, 0, 1).then_inc(sem["k6"], 1)
    g.affine_select(T.j1[:], T.onesf[:, 0:8], [[-16, 8]], op.is_ge, 0.0, 0, 1).then_inc(sem["k4"], 1)
    g.wait_ge(sem["k4"], 1)
    g.affine_select(T.jm[:], T.j1[:], [[16, 8]], op.is_ge, 0.0, 15, -1).then_inc(sem["k5"], 1)
    inc(v.memset(T.c16w[:], 16.0))
    for buf, top, bot in ((T.c16h, 16.0, 0.0), (T.onest, 1.0, 0.0), (T.onesb, 0.0, 1.0), (T.w64, 64.0, 1.0)):
        inc(v.memset(buf[0:64, :], top))
        inc(v.memset(buf[64:128, :], bot))
    inc(v.memset(T.fah[64:128, :], 0.0))
    inc(v.memset(T.fbh[64:128, :], 0.0))
    v.wait_ge(sem["k2"], 1)
    inc(v.tensor_scalar(T.hw[:], T.pi[:], 7, None, op.bitwise_and))
    inc(v.tensor_scalar(T.rw[:], T.pi[:], 3, None, op.logical_shift_right))
    inc(v.tensor_scalar(T.hh[:], T.pi[:], 3, None, op.bitwise_and))
    inc(v.tensor_scalar(T.rh[:], T.pi[:], 2, 15, op.logical_shift_right, op.bitwise_and))
    inc(v.tensor_scalar(T.pa[:], T.pi[:], 15, None, op.bitwise_and))
    v.wait_ge(sem["k3"], 1)
    inc(v.tensor_scalar(T.ji[:], T.ji[:], 15, None, op.bitwise_and))
    v.wait_ge(sem["k7"], 1)
    inc(v.tensor_copy(T.nof[:], T.ni[:]))
    flush()
    inc(v.tensor_scalar(T.faw[:], T.hw[:], 2048.0, None, op.mult))
    inc(v.tensor_copy(T.fbw[:], T.rw[:]))
    inc(v.tensor_scalar(T.fah[0:64, :], T.hh[0:64, :], 4096.0, None, op.mult))
    inc(v.tensor_copy(T.fbh[0:64, :], T.rh[0:64, :]))
    inc(v.tensor_copy(rhf, T.rh[:, 0:1]))
    inc(v.tensor_scalar(corr, T.pa[:, 0:1], 15.0, JUMP, op.not_equal, op.mult))
    inc(v.tensor_scalar(T.da[:], T.ji[:], 0.0, DROP, op.is_equal, op.mult))
    inc(v.tensor_scalar(T.db[:], T.ji[:], 15.0, JUMP, op.is_equal, op.mult))
    inc(v.tensor_scalar(T.e3f[:], T.ji[:], 0.0, None, op.is_equal))
    flush()
    inc(v.tensor_scalar(labw, T.hw[:, 0:1], 16.0, T.fbw[:, 0:1], op.mult, op.add))
    inc(v.tensor_scalar(codw, T.hw[:, 0:1], 2048.0, T.fbw[:, 0:1], op.mult, op.add))
    inc(v.tensor_scalar(labh, T.hh[:, 0:1], 16.0, rhf, op.mult, op.add))
    inc(v.tensor_tensor(T.d0[:], T.da[:], T.db[:], op.add))

    v.wait_ge(sem["k5"], 1)
    v.wait_ge(sem["k6"], 1)
    v.wait_ge(sem["st0"], n_st)
    inc(v.tensor_scalar(T.za[:], T.zi[:], 15, None, op.bitwise_and))
    inc(v.tensor_scalar(T.zb[:], T.zi[:], 7, 112, op.logical_shift_right, op.bitwise_and))
    inc(v.tensor_scalar(T.zc[:], T.zi[:], 4, 127, op.logical_shift_right, op.bitwise_and))
    flush()
    inc(v.tensor_tensor(T.zl[:], T.za[:], T.zb[:], op.add))
    for c in CHAINS:
        v.tensor_copy(T.woffs[:, O[c]], T.zc[:, O[c]]).then_inc(S("sof", c), 1)
    flush()
    v.tensor_tensor(T.gl[:], T.zl[:, 0:8].indirect(T.nof[:, 0:8]), T.ident[:], op.mult).then_inc(sem["sgl"], 1)

    def next_mask(t, c):
        lab = codw if t == 2 else labh if N - t in HALF else labw
        v.wait_ge(S("sxl", c), t)
        v.tensor_scalar(T.mask[:, J[c]], T["XL%d" % c][:, 0:64], lab, None, op.is_equal).then_inc(S("smk", c), 1)

    def state_spread(t):
        v.wait_ge(sem["scs"], t)
        v.tensor_tensor(T.us[:], T.CS[:, 0:8], T.jm[:], op.mult).then_inc(sem["sus"], 1)

    def offsets_out(t):
        v.wait_ge(sem["szs"], t)
        v.tensor_copy(T.zo[:, 8 * t - 8:8 * t], T.ZS[:, 0:8]).then_inc(sem["szo"], 1)

    for c in CHAINS:
        next_mask(1, c)
    for t in range(1, STEPS + 1):
        f = N - t
        a = 256 * f
        go = T["go%d" % (t % 2)]
        v.wait_ge(sem["map%d" % f], n_in)
        if t == 1:
            v.tensor_copy(T.m32[:], T.winu[:]).then_inc(sem["cv"], 1)
            v.wait_ge(sem["cv"], 1)
            v.tensor_scalar(T.c8[:], T.m32[:], 4, 127, op.logical_shift_right, op.bitwise_and).then_inc(sem["cv"], 1)
            v.tensor_scalar(T.a8[:], T.m32[:], 14351, None, op.bitwise_and).then_inc(sem["ca"], 1)
            v.wait_ge(sem["cv"], 2)
        for c in CHAINS:
            o = T.woffs[:, O[c]]
            mk = T.mask[:, J[c]]
            v.wait_ge(S("sof", c), t)
            v.wait_ge(S("smk", c), t)
            if t == 1:
                v.tensor_tensor(go[:, J[c]], T.c8[:, 0:128].indirect(o), mk, op.mult).then_inc(S("sgo", c), 1)
                v.wait_ge(sem["ca"], 1)
                v.tensor_tensor(T.gs[:, J[c]], T.a8[:, 0:128].indirect(o), mk, op.mult).then_inc(S("sgl", c), 1)
            elif f in HALF:
                v.tensor_tensor(go[:, J[c]], T.win[:, a:a + 256].indirect(o), mk, op.mult).then_inc(S("sgo", c), 1)
            else:
                v.tensor_tensor(go[:, J[c]], T.win[:, a:a + 128].indirect(o), mk, op.mult).then_inc(S("sgo", c), 1)
                v.tensor_tensor(T.gl[:, J[c]], T.win[:, a + 128:a + 256].indirect(o), mk,
                                op.mult).then_inc(S("sgl", c), 1)
        if t > 2:
            offsets_out(t - 2)
        if t > 1:
            state_spread(t - 1)
        for c in CHAINS:
            v.wait_ge(S("sc", c), t)
            v.tensor_tensor_scan(T.xs[:, J[c]], T.d0[:, J[c]], T["CB%d" % c][:, 0:64], 0.0, op.add,
                                 op.max).then_inc(S("ssc", c), 1)
        if t == STEPS:
            offsets_out(t - 1)
        for c in CHAINS:
            x = 64 * c
            if t < STEPS:
                next_mask(t + 1, c)
            v.wait_ge(S("ssc", c), t)
            if t < STEPS:
                v.tensor_scalar(T.woffs[:, O[c]], T.xs[:, x + 15:x + 64:16], corr, None,
                                op.subtract).then_inc(S("sof", c), 1)
            else:
                z = 8 * t - 8 + 4 * c
                v.tensor_scalar(T.zo[:, z:z + 4], T.xs[:, x + 15:x + 64:16], corr, None,
                                op.subtract).then_inc(sem["szo"], 1)

    pe.wait_ge(sem["k1"], 2)
    pe.wait_ge(sem["v"], nv[0])
    pe.wait_ge(sem["sgl"], 1)
    for c in CHAINS:
        pe.matmul(T["XL%d" % c][:, 0:64], T.ones[:], T.gl[:, J[c]], True, True).then_inc(S("sxl", c), 1)
    for t in range(1, STEPS + 1):
        f = N - t
        go = T["go%d" % (t % 2)]
        lhs = T.w64 if f == 1 else T.onest if f in HALF else T.ones
        for c in CHAINS:
            xl = T["XL%d" % c][:, 0:64]
            pe.wait_ge(S("sgo", c), t)
            pe.matmul(T["CB%d" % c][:, 0:64], lhs[:], go[:, J[c]], True, True).then_inc(S("sc", c), 1)
            if 1 < f and f in HALF:
                pe.matmul(xl, T.onesb[:], go[:, J[c]], True, True).then_inc(S("sxl", c), 1)
            elif f > 1:
                pe.wait_ge(S("sgl", c), t)
                lt, rt = (T.onesf, T.gs) if t == 1 else (T.ones, T.gl)
                pe.matmul(xl, lt[:], rt[:, J[c]], True, True).then_inc(S("sxl", c), 1)
        if t > 1:
            pe.wait_ge(sem["sus"], t - 1)
            if t > 2:
                pe.wait_ge(sem["szo"], t - 2)
            pe.matmul(T.ZS[:, 0:8], T.e3f[:], T.us[:], True, True).then_inc(sem["szs"], 1)
        if f > 1:
            fa, fb = (T.fah, T.fbh) if f - 1 in HALF else (T.faw, T.fbw)
            for c in CHAINS:
                pe.wait_ge(S("smk", c), t + 1)
            pe.matmul(T.CS[:, 0:8], go[:], T.c16h[:] if f in HALF else T.c16w[:], True, False)
            pe.matmul(T.CS[:, 0:8], T.mask[:], fa[:], False, False)
            pe.matmul(T.CS[:, 0:8], T.mask[:], fb[:], False, True).then_inc(sem["scs"], 1)

    sent, passed = [0], [0]

    def forward(f):
        g.wait_ge(sem["map%d" % f], n_in)
        m = topo.mask(core, team[1])
        g.remote_dma_fused([RemoteDMATransfer(dst_ids=[dst_id(topo, d) for d in team[1:]], dma_engine_mask=m,
                                              remote_sem=sem["map%d" % f], srcs=[window(T, f)],
                                              dsts=[window(T, f)] * (K - 1), alu_op=0)], local_sem=sem["fwd"])
        passed[0] += len(bits(m))

    if k == 0:
        for f in range(N - 1, N - 1 - AHEAD, -1):
            forward(f)
    for t in range(1, STEPS + 1):
        g.wait_ge(sem["szo"], t if t < STEPS else STEPS - 1 + len(CHAINS))
        dst = T.cores[N - 1 - t]
        m = topo.mask(core, dst)
        rid, pid, _ = topo.addr(dst)
        g.remote_dma(T.offs[:, 8 * w:8 * w + 8], T.zo[:, 8 * t - 8:8 * t], sem["lin"], sem["snt"], pid, rid, m)
        sent[0] += len(bits(m))
        f = N - AHEAD - t
        if k == 0 and f >= 1:
            forward(f)
    g.wait_ge(sem["snt"], sent[0])
    if passed[0]:
        g.wait_ge(sem["fwd"], passed[0])


def run_rank(g, core, rank, T, topo, teams):
    sem = T.sem
    v, a, sy = g.vector, g.scalar, g.sync
    op = AluOpType
    lister = rank < Q
    half = rank in HALF

    F = FIRST[rank]
    if lister:
        x = 8 * K * rank
        for i in range(8):
            e = sy if i % 2 else a
            e.dma_start(T.st8[16 * i:16 * i + 16, x:x + 8 * K], T.st[:, x:x + 8 * K]).then_inc(sem["lds"], 16)
    n_b = 0
    if half:
        for p in (0, 64):
            sy.dma_start(T.vb[p:p + 64, :], T.bp[:]).then_inc(sem["ldb"], 16)
        n_b = 32
    elif rank > 0:
        sy.dma_start(T.vb[:, 0:128], T.bp[:]).then_inc(sem["ldb"], 16)
        n_b = 16
    if lister:
        g.wait_ge(sem["lds"], 128)
        n = fused(g, core, topo, teams[rank], [T.st8[:, x + 8 * k:x + 8 * k + 8] for k in range(K)], [T.zi[:]] * K,
                  sem["st0"], sem["snl"])
        sy.wait_ge(sem["snl"], n)
    sy.dma_start(T.tabw[:, 0:F], T.tab[:, 0:F]).then_inc(sem["lda"], 16)
    n_t = 16
    if 0 < rank < HOLD:
        sy.dma_start(T.tabw[:, F:F + SECOND], T.tab[:, F:F + SECOND]).then_inc(sem["ldt"], 16)
        F += SECOND
        n_t = 32

    if rank > 0:
        if half:
            s_c, m_l = (4, 15) if rank > 1 else (6, 63)
            t_, b_ = slice(0, 64), slice(64, 128)
            src = T.wout[:]
            if rank > 1:
                v.memset(T.ty[t_, :], 0).then_inc(sem["v"], 1)
            v.wait_ge(sem["ldb"], n_b)
            v.tensor_scalar(T.tx[t_, :], T.vb[t_, :], s_c, 255, op.logical_shift_right, op.bitwise_and).then_inc(sem["v"], 1)
            v.tensor_scalar(T.tx[b_, :], T.vb[b_, :], m_l, None, op.bitwise_and).then_inc(sem["v"], 1)
            if rank > 1:
                v.tensor_scalar(T.ty[b_, :], T.vb[b_, :], 8, 48, op.logical_shift_right,
                                op.bitwise_and).then_inc(sem["v"], 1)
                v.wait_ge(sem["v"], 4)
                v.tensor_tensor(T.wout[:], T.tx[:], T.ty[:], op.add).then_inc(sem["enc"], 1)
            else:
                v.wait_ge(sem["v"], 2)
                v.tensor_copy(T.wout[:], T.tx[:]).then_inc(sem["enc"], 1)
            g.wait_ge(sem["enc"], 1)
        elif rank == N - 1:
            src = T.wu[:]
            v.wait_ge(sem["ldb"], n_b)
            v.tensor_copy(T.wu[:], T.vb[:, 0:128]).then_inc(sem["enc"], 1)
            g.wait_ge(sem["enc"], 1)
        else:
            src = T.wout[:]
            x, y = T.tx[:, 0:128], T.ty[:, 0:128]
            v.wait_ge(sem["ldb"], n_b)
            v.tensor_scalar(x, T.vb[:, 0:128], 15, None, op.bitwise_and).then_inc(sem["v"], 1)
            v.tensor_scalar(y, T.vb[:, 0:128], 8, 48, op.logical_shift_right, op.bitwise_and).then_inc(sem["v"], 1)
            v.tensor_scalar(T.tz[:], T.vb[:, 0:128], 4, 255, op.logical_shift_right, op.bitwise_and).then_inc(sem["v"], 1)
            v.wait_ge(sem["v"], 3)
            v.tensor_tensor(T.wout[:, 128:256], x, y, op.add).then_inc(sem["enc"], 1)
            v.tensor_copy(T.wout[:, 0:128], T.tz[:]).then_inc(sem["enc"], 1)
            g.wait_ge(sem["enc"], 2)
        if rank < HOLD:
            g.wait_ge(sem["lda"], 16)
        n = fused(g, core, topo, [t[0] for t in teams], [src] * Q, [window(T, rank)] * Q, sem["map%d" % rank], sem["snt"])
        sy.wait_ge(sem["snt"], n)

    sy.dma_start(T.tabw[:, F:], T.tab[:, F:]).then_inc(sem["ldt"], 16)

    if rank == N - 1:
        a.wait_ge(sem["snt"], n)
        for i in range(8):
            a.dma_start(T.st8[16 * i:16 * i + 16, :], T.st[:]).then_inc(sem["lds"], 16)
        v.wait_ge(sem["lds"], 128)
        v.tensor_copy(T.offs[:], T.st8[:]).then_inc(sem["ofr"], 1)
        got, n_in = sem["ofr"], 1
    else:
        got, n_in = sem["lin"], sum(len(bits(topo.mask(w, core))) for team in teams for w in team)

    n_p = len(PIECES)
    cut, x = [], 0
    for c in PIECES + PIECES:
        cut.append((x, x + c))
        x += c

    def part(i):
        x, y = cut[i]
        return T.yb[:, x:y], T.tabw[:, 0:16384].indirect(T.offs[:, x // 16:y // 16])

    for e in (v, a):
        e.wait_ge(sem["lda"], 16)
        e.wait_ge(sem["ldt"], n_t)
        e.wait_ge(got, n_in)
    for i in range(n_p):
        o, s = part(i)
        v.tensor_copy(o, s).then_inc(sem["yd%d" % i], 1)
    for i in range(n_p, 2 * n_p):
        o, s = part(i)
        a.activation(o, s, ActivationFunctionType.Copy).then_inc(sem["yd%d" % i], 1)
    for i in range(n_p):
        for j in (i, n_p + i):
            e = a if j == 2 * n_p - 1 else sy
            x, y = cut[j]
            e.wait_ge(sem["yd%d" % j], 1)
            e.dma_start(T.y[:, x:y], T.yb[:, x:y]).then_inc(sem["sto"], 16)
    sy.wait_ge(sem["sto"], 32 * n_p)
